import numpy as np, ml_dtypes
CORES = [6,15,38,47]
N = 4
import mx_ref
BF = ml_dtypes.bfloat16
def pick(q, e):
    c = np.concatenate([q[0].reshape(128, -1, 4), np.zeros((128, 1, 4), np.uint8)], axis=1); s = np.concatenate([q[1], np.ones((16, 1), np.uint8)], axis=1)
    return (np.ascontiguousarray(c[:, e].reshape(128, -1)), np.ascontiguousarray(s[:, e]))
def join(*qs):
    return (np.concatenate([q[0] for q in qs], axis=1), np.concatenate([q[1] for q in qs], axis=1))
def put(q, e, v):
    c, s = q[0].reshape(128, -1, 4).copy(), q[1].copy(); c[:, e] = v[0].reshape(128, -1, 4); s[:, e] = v[1]
    return (c.reshape(128, -1), s)
def pk(c, s):
    return (np.ascontiguousarray(c), mx_ref.live(s))
def emit(q):
    return q[0], q[1]
def cols(t, e):
    v = np.concatenate([t.reshape(128, -1, 4), np.zeros((128, 1, 4), BF)], axis=1)
    return np.ascontiguousarray(v[:, e]).reshape(128, -1)
def cut(t, i, w=512):
    return t[:, w * i:w * i + w]
def decode(q):
    o = []
    for b in range(4):
        e = np.zeros((128, 128, 4), np.float32); e[np.arange(128), np.arange(128), b] = 1
        o.append(mx_ref.matmul(mx_ref.quantize(e.reshape(128, 512).astype(BF)), q))
    return np.stack(o, axis=2).reshape(128, -1)
def f(rng, *shape):
    return mx_ref.flush((rng.standard_normal(shape, dtype=np.float32) * np.exp2(rng.integers(-2, 3, shape[:-1] + (1,)))).astype(BF))
def wide(rng, *shape, cols=0):
    v = rng.standard_normal(shape, dtype=np.float32) * np.exp2(rng.integers(-12, 13, shape)).astype(np.float32)
    if cols: v *= np.repeat(np.exp2(rng.integers(-cols, cols + 1, shape[:-2] + (1, shape[-1] // 4))) * (rng.random(shape[:-2] + (1, shape[-1] // 4)) > 0.0625), 4, axis=-1).astype(np.float32)
    return mx_ref.flush(v.astype(BF))
G, T, CAPP, R = 32, 192, 64, 3
def fit(v):
    v = np.array(v, np.float32)
    v[np.abs(v) < np.float32(2.0 ** -10)] = 0
    return v.astype(BF)
def plain(rng):
    return {"cb": fit(f(rng, N, 128, 4 * G)), "x": fit(f(rng, N, 128, 4 * R * T)), "w": f(rng, N, 128, 512)}
def part(rng, lab, k):
    s = (128, len(k), 4)
    v = np.where(k[None, :, None] == 2, rng.standard_normal(s), 1 + rng.random(s))
    return (v * (lab[:, None] == k[None, :])[:, :, None]).reshape(128, -1)
def setup_inputs(rng):
    return plain(rng)
def setup_inputs_crowd(rng):
    d = plain(rng)
    lab = rng.permutation(np.repeat([0, 1, 2], [40, 40, 48]))
    q, g = int(rng.integers(0, N - 2)), rng.permutation(G)[:2]
    home = int(rng.integers(0, R))
    rush = (home + 1 + int(rng.integers(0, R - 1))) % R
    cb = np.stack([part(rng, lab, np.full(G, 2)) for r in range(N)])
    k, size = np.zeros(G, int), np.full(G, 2.0 ** -6)
    k[g[1]] = 1
    size[g] = 1
    cb[q] = part(rng, lab, k) * np.repeat(size, 4)
    kinds = np.full((N, R, T), 2)
    for t in range(R):
        three, whole = np.sort(rng.permutation(N)[:3]), -1
        if t == home: three = np.concatenate([[q], np.sort(q + 1 + rng.permutation(N - 1 - q)[:2])])
        if t == rush:
            four, j = np.sort(rng.permutation(N)[:4]), int(rng.integers(0, 3))
            three, whole = np.delete(four, j), int(four[j])
        for s in range(N):
            more = int(rng.integers(1, T // 8 + 1))
            if s == three[0]: e = np.concatenate([np.zeros(CAPP, int), np.ones(more, int)])
            elif s == three[1]: e = np.concatenate([np.zeros(CAPP - 1, int), np.ones(1, int)])
            elif s == three[2]: e = np.concatenate([np.zeros(CAPP - 1, int), np.ones(1, int), rng.integers(0, 2, more)])
            elif s == whole: e = np.concatenate([np.zeros(CAPP, int), np.ones(T - CAPP, int)])
            else: e = np.zeros(int(rng.integers(CAPP // 2, CAPP + T // 8 + 1)), int)
            kinds[s, t, np.sort(rng.permutation(T)[:len(e)])] = e
    d["cb"], d["x"] = fit(cb), fit(np.stack([part(rng, lab, kinds[s].reshape(-1)) for s in range(N)]))
    return d
def setup_inputs_ties(rng):
    d = plain(rng)
    H = G // 2
    shared = fit(rng.standard_normal((128, 4 * H)))
    for r in range(N):
        both = np.concatenate([shared, fit(rng.standard_normal((128, 4 * H)))], axis=1)
        d["cb"][r] = cols(both, rng.permutation(np.concatenate([rng.integers(0, H, G - H), H + np.arange(H)])))
        v = cut(d["x"][r], 0, 4 * T).copy().reshape(128, T, 4)
        at = rng.permutation(T)
        v[:, at[:H]] = shared.reshape(128, H, 4)
        v[:, at[H:H + T // 16]] = 0
        d["x"][r] = np.concatenate([cols(v.reshape(128, -1), rng.permutation(T)) for t in range(R)], axis=1)
    return d
def setup_inputs_full(rng):
    d = plain(rng)
    at = rng.permutation(128)
    own = at[None, :] == np.arange(128)[:, None]
    cb = (1 + rng.random((128, 128, 4))) * np.where(own, 1.0, 2.0 ** -8)[:, :, None]
    kinds, who = np.zeros((N, R, T), int), np.arange(128) // G
    least, below = [], []
    for t in range(R):
        s, q = [int(v) for v in rng.permutation(N)[:2]]
        mine, free = np.flatnonzero(who == q), np.flatnonzero(who != q)
        if t == 0 or t == R - 1:
            least.append(int(rng.choice([v for v in free if G <= v < 128 - G and v not in least])))
            free = free[free != least[-1]]
            below.append((s + 1 + int(rng.integers(0, N - 1))) % N)
        for r in range(N):
            if r == s: kinds[r, t] = rng.permutation(np.concatenate([mine, mine, rng.choice(free, T - 2 * G)]))
            elif r < s: kinds[r, t] = rng.choice(free, T)
            else: kinds[r, t] = rng.choice(np.concatenate([free, mine]), T)
    x = np.zeros((N, 128, R * T, 4))
    for r in range(N):
        k = kinds[r].reshape(-1)
        x[r] = np.where(own[:, k][:, :, None], 1 + rng.random((128, R * T, 4)), (2 * rng.random((128, R * T, 4)) - 1) * 2.0 ** -7)
    x[below[0]][:, :2] = -(1 + rng.random((128, 2, 4))) * np.where(own[:, least[0]], 2.0 ** -9, 2.0 ** -6)[:, None, None]
    size = np.where(own[:, least[1]], 2.0 ** 15, np.where(own[:, least[0]], 2.0 ** 24, 2.0 ** 21))
    i = (R - 1) * T
    x[below[1]][:, i:i + 2] = -(3 + rng.random((128, 2, 4))) * size[:, None, None]
    d["cb"] = fit(np.stack([cb[:, G * r:G * r + G].reshape(128, -1) for r in range(N)]))
    d["x"] = fit(x.reshape(N, 128, -1))
    return d
def setup_inputs_idle(rng):
    d = plain(rng)
    q, own = int(rng.integers(0, N)), rng.permutation(128) < 64
    cb = rng.standard_normal((N, 128, 4 * G))
    for r in range(N): cb[r] *= (own if r == q else ~own)[:, None]
    early = np.arange(4 * R * T) < 4 * (R - 1) * T
    d["cb"], d["x"] = fit(cb), fit(d["x"].astype(np.float32) * ~(own[:, None] & early[None, :]))
    return d
def setup_inputs_spread(rng):
    d = plain(rng)
    d["cb"] = fit(wide(rng, N, 128, 4 * G).astype(np.float32) * 64)
    d["x"] = fit(wide(rng, N, 128, 4 * R * T, cols=4).astype(np.float32) * 64)
    return d
def check_inputs(d):
    b = []
    for k, lo, hi in (("cb", -10, 28), ("x", -10, 28), ("w", -30, 30)):
        v = np.abs(d[k].astype(np.float32))
        if not (np.isfinite(v).all() and ((v == 0) | (v >= 2.0 ** lo) & (v <= 2.0 ** hi)).all()): b.append("a value of " + k)
    return b
def admitted(win):
    a = np.full((2, 128), -1)
    for s in range(N):
        n = np.zeros(N, int)
        for i in range(T):
            k = win[T * s + i]
            n[k // G] += 1
            if n[k // G] > CAPP: continue
            if a[0, k] < 0: a[0, k] = T * s + i
            elif a[1, k] < 0: a[1, k] = T * s + i
    return a
def reference(cb, x, w):
    y, ids = np.zeros((N, 128, R * 2 * G), np.float32), np.zeros((N, 1, R * 2 * G), np.float32)
    oc, osc = np.zeros((N, 128, 4 * G), np.uint8), np.zeros((N, 16, G), np.uint8)
    half, quarter = np.float32(0.5), np.float32(0.25)
    qw = [mx_ref.quantize(np.ascontiguousarray(w[r])) for r in range(N)]
    c = join(*[mx_ref.quantize(np.ascontiguousarray(cb[r])) for r in range(N)])
    for t in range(R):
        tok = join(*[mx_ref.quantize(np.ascontiguousarray(cut(x[s], t, 4 * T))) for s in range(N)])
        a = admitted(np.argmax(mx_ref.matmul(c, tok) + np.float32(0), axis=0))
        for r in range(N):
            e = a[:, G * r:G * r + G].T.reshape(-1)
            i = t * 2 * G
            y[r, :, i:i + 2 * G] = mx_ref.matmul(qw[r], pick(tok, e))
            ids[r, 0, i:i + 2 * G] = e
        v = decode(join(c, pick(tok, a[0]), pick(tok, a[1]))).reshape(128, 3, 128, 4)
        one = half * v[:, 0] + half * v[:, 1]
        two = half * v[:, 0] + (quarter * v[:, 1] + quarter * v[:, 2])
        new = np.where((a[1] >= 0)[None, :, None], two, one).reshape(128, 512).astype(BF)
        moved = np.flatnonzero(a[0] >= 0)
        c = put(c, moved, pick(mx_ref.quantize(np.ascontiguousarray(new)), moved))
    for r in range(N):
        oc[r], osc[r] = emit(pick(c, np.arange(G * r, G * r + G)))
    return {"y": y, "ids": ids, "oc": oc, "osc": osc}

@@ -1,0 +1,500 @@
+from concourse.bass import DstId, RemoteDMATransfer
+from concourse.mybir import dt, AluOpType as A, ActivationFunctionType as AF
+
+CODE = "float8_e4m3fn_x4"
+N, G, TOK, R, CAPP = 4, 32, 192, 3, 64
+UNIT = 2.0 ** -18
+WIN = 512
+FAR = 64.0
+LOW = -1.0e29
+LIFT = 1024.0
+
+SCRATCH = {
+    "cbt": ("sbuf", [128, 768], "bfloat16"), "xt": ("sbuf", [128, 2304], "bfloat16"), "wt": ("sbuf", [128, 512], "bfloat16"),
+    "pt": ("sbuf", [128, 512], "bfloat16"), "zz": ("sbuf", [128, 512], "bfloat16"),
+    "ptx": ("sbuf", [128, 512], "bfloat16"), "zzx": ("sbuf", [128, 512], "bfloat16"),
+    "nt": ("sbuf", [128, 512], "bfloat16"), "ct": ("sbuf", [128, 2048], "bfloat16"), "et": ("sbuf", [128, 2048], "bfloat16"),
+    "idf": ("sbuf", [128, 4], "float32"), "ps": ("psum", [128, 4096], "float32"),
+}
+for _c, _s, _n in (("cq", "cqs", 512), ("eq", "eqs", 512), ("cbq", "cbs", 128), ("xq", "xs", 576), ("wq", "ws", 128),
+                   ("pq", "pqs", 128), ("zq", "zqs", 128), ("pxq", "pxs", 128), ("zxq", "zxs", 128), ("adm", "adms", 160),
+                   ("ady", "adys", 128)):
+    SCRATCH[_c] = ("sbuf", [128, _n], CODE)
+    SCRATCH[_s] = ("sbuf", [128, _n], "uint8")
+for _b in ("rowi", "k16", "negc", "ma", "mb", "msk", "ls1", "ls2", "dist", "hc", "s4", "hh"):
+    SCRATCH[_b] = ("sbuf", [128, 128], "float32")
+for _b in ("pcol", "npcol", "qcol", "corr", "ncorr"):
+    SCRATCH[_b] = ("sbuf", [128, 1], "float32")
+for _b in ("dd", "ab", "mx", "sec", "junk"):
+    SCRATCH[_b] = ("sbuf", [128, 32], "float32")
+for _b, _n, _d in (("pi", 1, "int32"), ("qi", 1, "int32"), ("ii", 16, "float32"), ("hold", 16, "float32"), ("cut", 16, "float32"),
+                   ("flag", 16, "float32"), ("lst", 16, "uint16"), ("cs", 2, "float32"), ("v2", 2, "float32"),
+                   ("f5", 2, "float32"), ("alst", 6, "uint16"), ("mv", 2, "float32"), ("clst", 2, "uint16"),
+                   ("ilst", 2, "uint16"), ("gnew", 2, "float32"), ("vi", 4, "int32"), ("iv", 4, "int32"), ("sv", 4, "int32"),
+                   ("s192", 4, "float32"), ("sg", 4, "float32"), ("wv", 4, "float32")):
+    SCRATCH[_b] = ("sbuf", [128, _n], _d)
+for _t in range(R):
+    SCRATCH["meta%d" % _t] = ("sbuf", [128, 16], "bfloat16")
+    SCRATCH["lm%d" % _t] = ("sbuf", [128, 20], "bfloat16")
+    SCRATCH["snd%d" % _t] = ("sbuf", [128, 192], CODE)
+    SCRATCH["sns%d" % _t] = ("sbuf", [128, 192], "uint8")
+    SCRATCH["land%d" % _t] = ("sbuf", [128, 640], CODE)
+    SCRATCH["lans%d" % _t] = ("sbuf", [128, 640], "uint8")
+    SCRATCH["yo%d" % _t] = ("sbuf", [128, 64], "float32")
+    SCRATCH["ido%d" % _t] = ("sbuf", [128, 4], "float32")
+for _t in range(R + 1):
+    SCRATCH["ca%d" % _t] = ("sbuf", [128, 256], CODE)
+    SCRATCH["cas%d" % _t] = ("sbuf", [128, 256], "uint8")
+SEMAPHORES = ["qv", "qs", "qt", "qp", "ldcb", "ldx0", "ldx1", "ldx2", "ldw", "st", "sent",
+              "arc0", "arc1", "arc2", "arm0", "arm1", "arm2", "ark0", "ark1", "ark2"]
+
+
+def rank_program(g, core, T, topo):
+    rank = T.rank_of(core)
+    if rank is None:
+        return
+    cores = list(T.cores)
+
+    def others(r):
+        def hops(d):
+            a, b = topo.chip(cores[r]), topo.chip(cores[d])
+            return 0 if a == b else (1 if topo.mates(a, b) or topo.same_plane(a, b) else 2)
+        return sorted([d for d in range(N) if d != r], key=lambda d: -hops(d))
+
+    def bits(es):
+        m = 0
+        for e in es:
+            m |= 1 << e
+        return m
+
+    def common(r):
+        es = topo.engines(cores[r], cores[others(r)[0]])
+        for d in others(r):
+            es = [e for e in es if e in topo.engines(cores[r], cores[d])]
+        return es
+
+    def split(r, kind):
+        es = common(r)
+        h, q = len(es) // 2, len(es) // 4
+        a, b, c = others(r)
+        if kind == 0:
+            return {a: es[:h], b: es[h:h + q], c: es[h + q:]}
+        return {a: es[h:], b: es[:q], c: es[q:h]}
+
+    oth = others(rank)
+    full = common(rank)
+    dst = {}
+    for d in oth:
+        rid, pid, _ = topo.addr(cores[d])
+        dst[d] = (rid, pid)
+    n_meta = sum(len(split(s, 0)[rank]) for s in range(N) if s != rank)
+    n_tok = sum(len(split(s, 1)[rank]) + len(common(s)) for s in range(N) if s != rank)
+    n_cen = sum(2 * len(common(s)) for s in range(N) if s != rank)
+
+    ENG = {"v": g.vector, "s": g.scalar, "t": g.tensor, "p": g, "y": g.sync}
+    cnt = {}
+    know = {q: {} for q in ENG}
+    writers, readers = {}, {}
+
+    def await_(q, recs):
+        recs = [r for r in recs if know[q].get(r[0], 0) < r[1]]
+        keep = []
+        for i, r in enumerate(recs):
+            if any(o is not r and o[2].get(r[0], 0) >= r[1] and not (o[0] == r[0] and o[1] == r[1] and j > i)
+                   for j, o in enumerate(recs)):
+                continue
+            keep.append(r)
+        for r in keep:
+            if know[q].get(r[0], 0) < r[1]:
+                ENG[q].wait_ge(T.sem[r[0]], r[1])
+            for k, v in r[2].items():
+                know[q][k] = max(know[q].get(k, 0), v)
+        for r in recs:
+            for k, v in r[2].items():
+                know[q][k] = max(know[q].get(k, 0), v)
+
+    def deps(q, rd, wr):
+        recs = []
+        for k in rd:
+            recs += [r for r in writers.get(k, [])]
+            if k[:2] == "ps":
+                recs += [r for r in readers.get(k, []) if r[3] != q]
+        for k in wr:
+            recs += writers.get(k, []) + readers.get(k, [])
+        return recs
+
+    def note(rec, rd, wr):
+        for k in wr:
+            writers[k], readers[k] = [rec], []
+        for k in rd:
+            if k not in wr:
+                readers.setdefault(k, []).append(rec)
+
+    def record(q, sem, n):
+        cnt[sem] = cnt.get(sem, 0) + n
+        clk = dict(know[q])
+        clk[sem] = cnt[sem]
+        return (sem, cnt[sem], clk, q)
+
+    def run(q, f, rd, wr):
+        await_(q, deps(q, rd, wr))
+        f(ENG[q]).then_inc(T.sem["q" + q], 1)
+        note(record(q, "q" + q, 1), rd, wr)
+
+    def dma(q, out, in_, rd, wr, sem):
+        await_(q, deps(q, rd, wr))
+        ENG[q].dma_start(out, in_).then_inc(T.sem[sem], 16)
+        note(record(q, sem, 16), rd, wr)
+
+    def arrive(sem, n, keys):
+        cnt[sem] = n
+        rec = (sem, n, {sem: n}, "r")
+        for k in keys:
+            writers.setdefault(k, []).append(rec)
+
+    def remote(transfers, rd):
+        await_("p", deps("p", rd, []))
+        g.remote_dma_fused([t for t, _ in transfers], local_sem=T.sem["sent"])
+        cnt["sent"] = cnt.get("sent", 0) + sum(n for _, n in transfers)
+
+    def one(d, src, to, sem, es):
+        return (RemoteDMATransfer(dst_ids=[DstId(rid=dst[d][0], pnc=dst[d][1])], dma_engine_mask=bits(es),
+                                  remote_sem=T.sem[sem], src=src, dst=to), len(es))
+
+    def many(src, to, sem):
+        return (RemoteDMATransfer(dst_ids=[DstId(rid=dst[d][0], pnc=dst[d][1]) for d in oth], dma_engine_mask=bits(full),
+                                  remote_sem=T.sem[sem], srcs=[src], dsts=[to for d in oth]), len(full))
+
+    def ts(out, in0, s1, s2, o0, o1, rd, wr):
+        if o1 is None:
+            run("v", lambda e: e.tensor_scalar(out, in0, s1, None, o0), rd, wr)
+        else:
+            run("v", lambda e: e.tensor_scalar(out, in0, s1, s2, o0, o1), rd, wr)
+
+    def tt(out, a, b, op, rd, wr):
+        run("v", lambda e: e.tensor_tensor(out, a, b, op), rd, wr)
+
+    def scan(out, a, b, first, o0, o1, rd, wr):
+        run("v", lambda e: e.tensor_tensor_scan(out, a, b, first, o0, o1), rd, wr)
+
+    def act(out, in_, func, bias, scale, rd, wr, total=None):
+        run("s", lambda e: e.activation(out, in_, func, bias=bias, scale=scale, accum_out=total), rd, wr)
+
+    def fill(ap, c, key):
+        run("v", lambda e: e.memset(ap, c), [], [key])
+
+    def flat(out, in_, c, rd, key):
+        act(out, in_, AF.Identity, c, 0.0, rd, [key])
+
+    def quant(c, s, a, b, tile, x, keys, out):
+        run("v", lambda e: e.quantize_mx(T[c][:, a:b], T[s][:, a:b], T[tile][:, x:x + 4 * (b - a)]), keys, out)
+
+    def mm(bank, l, la, r, ras, rd):
+        lc, lsc = l
+        rc, rs = r
+        await_("t", deps("t", rd, ["ps%d" % bank]))
+        for i, ra in enumerate(ras):
+            call = g.tensor.matmul_mx(T.ps[:, 512 * bank:512 * bank + 128], T[lc][:, la:la + 128], T[lsc][:, la:la + 128],
+                                      T[rc][:, ra:ra + 128], T[rs][:, ra:ra + 128], i == 0, i == len(ras) - 1)
+        call.then_inc(T.sem["qt"], 1)
+        note(record("t", "qt", 1), rd, ["ps%d" % bank])
+
+    def pick(kind, dstb, da, n, srcb, sa, sb, lstb, la, rd, wr):
+        k = n // 16
+        if kind == "c":
+            run("v", lambda e: e.tensor_copy(T[dstb][:, da:da + n].bitcast(dt.uint32),
+                                             T[srcb][:, sa:sb].bitcast(dt.uint32).indirect(T[lstb][:, la:la + k])), rd, wr)
+        else:
+            run("s", lambda e: e.activation(T[dstb][:, da:da + n],
+                                            T[srcb][:, sa:sb].indirect(T[lstb][:, la:la + k]), AF.Copy), rd, wr)
+
+    def iota(out, pattern, base, mult, key, imprecise=True):
+        if imprecise:
+            run("p", lambda e: e.iota(out, pattern, base, mult, allow_small_or_imprecise_dtypes=True), [], [key])
+        else:
+            run("p", lambda e: e.iota(out, pattern, base, mult), [], [key])
+
+    def ps(bank, a, b, p0=0):
+        return T.ps[p0:128, 512 * bank + a:512 * bank + b]
+
+    dma("y", T.cbt[:, 0:128], T.cb[:, :], [], ["cbt"], "ldcb")
+    dma("y", T.xt[:, 0:768], T.x[:, 0:768], [], ["xt0"], "ldx0")
+
+    iota(T.pi[:, :], [[1, 1]], 0, 1, "pi", False)
+    iota(T.rowi[:, :], [[1, 128]], 0, 0, "rowi")
+    iota(T.pcol[:, :], [[1, 1]], 0, 1, "pcol")
+    iota(T.npcol[:, :], [[1, 1]], 0, -1, "npcol")
+    iota(T.k16[:, :], [[0, 8], [1, 16]], 0, 0, "k16")
+    fill(T.et[:, :], 0.0, "etz")
+    fill(T.cbt[:, 128:768], 0.0, "cbtz")
+    ts(T.qi[:, :], T.pi[:, :], 15, None, A.bitwise_and, None, ["pi"], ["qi"])
+    run("v", lambda e: e.tensor_copy(T.qcol[:, :], T.qi[:, :]), ["qi"], ["qcol"])
+    for h in range(2):
+        ts(T.ilst[:, h:h + 1], T.qcol[:, :], 16.0 * h, None, A.add, None, ["qcol"], ["ilst%d" % h])
+    for key, sl, c in (("ct0c", slice(1, 512, 4), 0.0), ("ct0d", slice(3, 512, 4), 0.0), ("ct1a", slice(512, 1024, 4), 1.0),
+                       ("ct1b", slice(514, 1024, 4), -1.0)):
+        flat(T.ct[:, sl], T.rowi[:, :], c, ["rowi"], key)
+
+    quant("cbq", "cbs", 0, 128, "cbt", 0, ["cbt", "cbtz"], ["cbq"])
+    own = slice(G * rank, G * rank + G)
+    remote([many(T.cbq[:, 0:G].bitcast(dt.uint8), T.ca0[:, own].bitcast(dt.uint8), "arc0")], ["cbq"])
+    remote([many(T.cbs[:, 0:G], T.cas0[:, own], "arc0")], ["cbq"])
+    pick("c", "ca0", G * rank, G, "cbq", 0, 128, "ilst", 0, ["cbq", "ilst0", "ilst1"], ["ca0"])
+    pick("s", "cas0", G * rank, G, "cbs", 0, 128, "ilst", 0, ["cbq", "ilst0", "ilst1"], ["cas0"])
+    arrive("arc0", n_cen, ["ca0", "cas0"])
+    iota(T.ptx[:, :], [[0, 512]], 0, 0, "ptx")
+    iota(T.zzx[:, :], [[0, 512]], 0, 0, "zzx")
+    iota(T.hold[:, :], [[0, 4], [1, 4]], 0, 0, "hold")
+    for i, c in enumerate((1.0, 1.0, 0.0, 0.0)):
+        flat(T.ct[:, 1024 + i:1536:4], T.rowi[:, :], c, ["rowi"], "ct2%d" % i)
+    fill(T.negc[:, :], LOW, "negc")
+    ts(T.ct[:, 0:512:4], T.rowi[:, :], T.pcol[:, :], None, A.is_ge, None, ["rowi", "pcol"], ["ct0a"])
+    ts(T.ct[:, 2:512:4], T.rowi[:, :], T.pcol[:, :], -1.0, A.is_ge, A.mult, ["rowi", "pcol"], ["ct0b"])
+    for i, c in enumerate((0.0, -1.0, 1.0, 1.0)):
+        fill(T.ct[:, 1536 + i:2048:4], c, "ct3%d" % i)
+    ts(T.ct[64:128, 513:1024:4], T.rowi[64:128, :], T.pcol[64:128, :], None, A.is_ge, None, ["rowi", "pcol"], ["ct1c"])
+    ts(T.ct[64:128, 515:1024:4], T.rowi[64:128, :], T.pcol[64:128, :], -1.0, A.is_ge, A.mult, ["rowi", "pcol"], ["ct1d"])
+    fill(T.ct[0:64, 513:1024:4], 0.0, "ct1e")
+    fill(T.ct[0:64, 515:1024:4], 0.0, "ct1f")
+    fill(T.pt[:, :], 0.0, "pt")
+    fill(T.zz[0:64, 1:512:4], 0.0, "zza")
+    fill(T.zz[0:64, 3:512:4], 0.0, "zzb")
+    fill(T.pt[:, 0:1], 1.0, "pt")
+    fill(T.pt[64:128, 1:2], 1.0, "pt")
+    quant("cq", "cqs", 0, 512, "ct", 0, ["ct0a", "ct0b", "ct0c", "ct0d", "ct1a", "ct1b", "ct1c", "ct1d", "ct1e", "ct1f"]
+          + ["ct%d%d" % (b, i) for b in (2, 3) for i in range(4)], ["cq"])
+    ts(T.msk[:, :], T.k16[:, :], T.qcol[:, :], -33.0 * LIFT, A.is_equal, A.mult, ["k16", "qcol"], ["msk"])
+    ts(T.corr[:, :], T.qcol[:, :], -LIFT, 15.0 * LIFT, A.mult, A.add, ["qcol"], ["corr"])
+    quant("xq", "xs", 0, 192, "xt", 0, ["xt0"], ["xq0"])
+    ts(T.msk[:, :], T.msk[:, :], LIFT, None, A.add, None, [], ["msk"])
+    ts(T.ncorr[:, :], T.corr[:, :], -UNIT, None, A.mult, None, ["corr"], ["ncorr"])
+    fill(T.ptx[:, 0:1], 1.0, "ptx")
+    fill(T.ptx[64:128, 1:2], 1.0, "ptx")
+    act(T.dist[:, :], T.rowi[:, :], AF.Abs, T.npcol[:, 0:1], 1.0, ["rowi", "npcol"], ["dist"])
+    for b in range(4):
+        act(T.et[:, 512 * b + b:512 * b + 512:4], T.dist[:, :], AF.Relu, 0.25, -0.25, ["dist", "etz"], ["et%d" % b])
+    await_("y", writers["ca0"])
+    dma("y", T.wt[:, :], T.w[:, :], [], ["wt"], "ldw")
+    dma("y", T.xt[:, 768:1536], T.x[:, 768:1536], [], ["xt1"], "ldx1")
+
+    def zero_block(t):
+        quant("land%d" % t, "lans%d" % t, WIN, WIN + 128, "cbt", 128, ["cbtz"], ["lz%d" % t])
+
+    def late_constants():
+        flat(T.nt[:, :], T.cbt[:, 128:640], 0.0, ["cbtz"], "nt")
+        for h in range(2):
+            ts(T.gnew[:, h:h + 1], T.qcol[:, :], 128.0 + 16 * h, None, A.add, None, ["qcol"], ["gnew%d" % h])
+        quant("adm", "adms", 0, 160, "cbt", 128, ["cbtz"], ["adm", "adms"])
+        zero_block(0)
+
+    XQ, CQ, EQ = ("xq", "xs"), ("cq", "cqs"), ("eq", "eqs")
+    for t in range(R):
+        last = t == R - 1
+        ca, cas = "ca%d" % t, "cas%d" % t
+        CA = (ca, cas)
+        lm, meta, yo, ido = T["lm%d" % t], T["meta%d" % t], T["yo%d" % t], T["ido%d" % t]
+        land, lans, snd, sns = "land%d" % t, "lans%d" % t, "snd%d" % t, "sns%d" % t
+        mm(0, XQ, 192 * t, CA, (0,), ["xq%d" % t, ca, cas])
+        mm(1, XQ, 192 * t + 64, CA, (0,), ["xq%d" % t, ca, cas])
+        scan(T.ma[:, :], ps(0, 0, 128), T.negc[:, :], LOW, A.max, A.max, ["ps0", "negc"], ["ma"])
+        scan(T.mb[64:128, :], ps(1, 0, 128, 64), T.negc[64:128, :], LOW, A.max, A.max, ["ps1", "negc"], ["mb"])
+
+        def before(q, out, m, key, p0, k0, k1, step, wr):
+            if q == "v":
+                ts(out, m[p0:128, k0:k1:step], m[p0:128, 127:128], None, A.is_lt, None, [key], [wr])
+            else:
+                act(out, m[p0:128, k0:k1:step], AF.Sign, m[p0:128, 127:128], -1.0, [key], [wr])
+        if t == 0:
+            await_("s", writers["pt"] + writers["ptx"])
+            await_("v", writers["pt"] + writers["ptx"])
+        before("s", T.pt[:, 4:512:4], T.ma, "ma", 0, 0, 127, 1, "pt0")
+        before("s", T.pt[:, 2:512:4], T.ma, "ma", 0, 0, 128, 1, "pt2")
+        before("v", T.pt[64:128, 5:512:4], T.mb, "mb", 64, 0, 127, 1, "pt1")
+        before("v", T.pt[64:128, 3:512:4], T.mb, "mb", 64, 0, 128, 1, "pt3")
+        before("v", T.ptx[64:128, 5:14:4], T.mb, "mb", 64, 31, 96, 32, "px1")
+        before("v", T.ptx[64:128, 3:12:4], T.mb, "mb", 64, 31, 96, 32, "px3")
+        quant("pq", "pqs", 0, 128, "pt", 0, ["pt", "pt0", "pt1", "pt2", "pt3"], ["pq"])
+        before("s", T.ptx[:, 4:13:4], T.ma, "ma", 0, 31, 96, 32, "px0")
+        before("s", T.ptx[:, 2:11:4], T.ma, "ma", 0, 31, 96, 32, "px2")
+        mm(3, CQ, 128, ("pq", "pqs"), (0,), ["cq", "pq"])
+        mm(2, CQ, 0, ("pq", "pqs"), (0,), ["cq", "pq"])
+        quant("pxq", "pxs", 0, 128, "ptx", 0, ["ptx", "px0", "px1", "px2", "px3"], ["pxq"])
+        mm(6, CQ, 0, ("pxq", "pxs"), (0,), ["cq", "pxq"])
+        mm(7, CQ, 128, ("pxq", "pxs"), (0,), ["cq", "pxq"])
+        for el, c in ((1, 1.0), (3, 2.0)):
+            act(T.zz[64:128, el:512:4], ps(3, 0, 128, 64), AF.Relu, c, -1.0, ["ps3"], ["zz%d" % el])
+        for el, c in ((0, 1.0), (2, 2.0)):
+            ts(T.zz[:, el:512:4], ps(2, 0, 128), c, None, A.is_lt, None, ["ps2"], ["zz%d" % el])
+        quant("zq", "zqs", 0, 128, "zz", 0, ["zza", "zzb", "zz0", "zz1", "zz2", "zz3"], ["zq"])
+        mm(4, CQ, 256, ("zq", "zqs"), (0,), ["cq", "zq"])
+        mm(5, CQ, 384, ("zq", "zqs"), (0,), ["cq", "zq"])
+        for el, bank, p0 in ((0, 6, 0), (1, 7, 64)):
+            ts(T.zzx[p0:128, el:64:16], ps(bank, 0, 4, p0), CAPP + 1.0, UNIT, A.is_lt, A.mult, ["ps%d" % bank, "zzx"], ["zx%d" % el])
+        quant("zxq", "zxs", 0, 128, "zzx", 0, ["zzx", "zx0", "zx1"], ["zxq"])
+        mm(0, CQ, 256, ("zxq", "zxs"), (0,), ["cq", "zxq"])
+        for j, ls in ((0, T.ls1), (1, T.ls2)):
+            scan(ls[:, :], T.msk[:, :], ps(4 + j, 0, 128), 0.0, A.add, A.max, ["ps%d" % (4 + j), "msk"], ["ls%d" % j])
+        for j, ls in ((0, T.ls1), (1, T.ls2)):
+            for h in range(2):
+                act(T.ii[:, 2 * j + h:16:4], ls[:, 15 + 16 * h:128:32], AF.Identity, T.ncorr[:, 0:1], UNIT, ["ls%d" % j, "ncorr"],
+                    ["ii%d%d" % (j, h)])
+            ts(T.lst[:, j:16:2], ls[:, 15:128:16], T.corr[:, 0:1], float(TOK - 1), A.subtract, A.min,
+               ["ls%d" % j, "corr"], ["lst%d" % j])
+        II = ["ii00", "ii01", "ii10", "ii11"]
+        LST = ["lst0", "lst1"]
+        mk = "meta%d" % t
+        sp0, sp1 = split(rank, 0), split(rank, 1)
+        me = slice(64 * rank, 64 * rank + 64)
+
+        def slots(kind, n):
+            d = (oth + [rank])[n]
+            b, x = (snd, "xq") if kind == "c" else (sns, "xs")
+            o = land if kind == "c" else lans
+            if n < 3:
+                pick(kind, b, 64 * n, 64, x, 192 * t, 192 * t + 192, "lst", 4 * d, LST + ["xq%d" % t], ["%s.%d" % (b, n)])
+            else:
+                pick(kind, o, 64 * rank, 64, x, 192 * t, 192 * t + 192, "lst", 4 * d, LST + ["xq%d" % t], [o])
+
+        def send_codes(n):
+            remote([one(oth[n], T[snd][:, 64 * n:64 * n + 64].bitcast(dt.uint8), T[land][:, me].bitcast(dt.uint8), "ark%d" % t, full)],
+                   ["%s.%d" % (snd, n)])
+
+        def place(d):
+            e = [s for s in range(N) if s != d].index(rank)
+            return slice(8 + 4 * e, 12 + 4 * e)
+        for n in range(4):
+            slots("s", n)
+        scan(T.cut[:, :], T.hold[:, :], ps(0, 0, 16), 0.0, A.min, A.add, ["hold", "ps0"], ["cut"])
+        slots("c", 0)
+        send_codes(0)
+        tt(T.flag[:, :], T.ii[:, :], T.cut[:, :], A.is_ge, II + ["cut"], ["flag"])
+        slots("c", 1)
+        tt(meta[:, :], T.ii[:, :], T.flag[:, :], A.add, II + ["flag"], [mk])
+        remote([one(d, meta[:, 4 * d:4 * d + 4], lm[:, place(d)], "arm%d" % t, sp0[d]) for d in oth], [mk])
+        send_codes(1)
+        slots("c", 2)
+        remote([one(e, T[sns][:, 64 * m:64 * m + 64], T[lans][:, me], "ark%d" % t, sp1[e]) for m, e in enumerate(oth)],
+               ["%s.%d" % (sns, m) for m in range(3)])
+        send_codes(2)
+        slots("c", 3)
+        if t == 0:
+            quant("eq", "eqs", 0, 512, "et", 0, ["etz"] + ["et%d" % b for b in range(4)], ["eq"])
+            o = [rank] + [s for s in range(N) if s != rank]
+            steps = [-16, 0, 0, 64 * (o[0] - o[1]) + 16, -16, 64 * (o[1] - o[2]) + 16, -16, 64 * (o[2] - o[3]) + 16, -16]
+            fill(T.dd[:, 0:20], -16.0 / 512, "dd")
+            for i, c in enumerate(steps):
+                if c != -16:
+                    run("v", lambda e: e.memset(T.dd[:, i:20:10], c / 512), ["dd"], ["dd%d" % i])
+            for h in range(2):
+                ts(T.dd[:, 10 * h + 9:10 * h + 10], T.qcol[:, :], 64.0 * o[3] + 16 + 32 * h, 1.0 / 512, A.add, A.mult,
+                   ["qcol", "dd"], ["dq%d" % h])
+            fill(T.ab[:, 0:2], FAR, "ab0")
+        for b in range(4):
+            mm(4 + b, EQ, 128 * b, CA, (0,), ["eq", ca, cas])
+        for b in range(4):
+            act(T.hc[:, 32 * b:32 * b + 32], ps(4 + b, G * rank, G * rank + G), AF.Copy, 0.0, 2.0, ["ps%d" % (4 + b)], ["hc%d" % b])
+        fill(lm[:, 4:8], 8.0, "lp%d" % t)
+        run("v", lambda e: e.tensor_copy(lm[:, 0:4], meta[:, 4 * rank:4 * rank + 4]), [mk], ["lo%d" % t])
+        if t == 0:
+            late_constants()
+        arrive("arm%d" % t, n_meta, ["lm%d" % t])
+        LM = ["lm%d" % t, "lo%d" % t, "lp%d" % t]
+        DD = ["dd", "dq0", "dq1"] + ["dd%d" % i for i in (1, 2, 3, 5, 7)]
+        for h in range(2):
+            scan(T.ab[:, 2 + h:22:2], lm[:, h:20:2], T.dd[:, 10 * h:10 * h + 10], FAR, A.min, A.add, LM + DD, ["ab%d" % (1 + h)])
+        for h in range(2):
+            act(T.junk[:, 10 * h:10 * h + 10], lm[:, h:20:2], AF.Sign, 0.75, -1.0, LM, ["cs%d" % h], T.cs[:, h:h + 1])
+        tt(T.mx[:, 0:20], lm[:, :], T.ab[:, 0:20], A.max, LM + ["ab0", "ab1", "ab2"], ["mx"])
+        F, S = T.ab[:, 20:22], T.sec[:, 9:20:10]
+        ts(T.f5[:, :], F, 512.0, None, A.mult, None, ["ab1", "ab2"], ["f5"])
+        for h in range(2):
+            scan(T.sec[:, 10 * h:10 * h + 10], T.mx[:, h:20:2], T.dd[:, 10 * h:10 * h + 10], FAR, A.min, A.add, ["mx"] + DD, ["sc%d" % h])
+        ts(T.alst[:, 2:4], F, 512.0, None, A.mult, None, ["ab1", "ab2"], ["alst1"])
+        ts(T.v2[:, :], T.cs[:, :], -7.0, 512.0, A.is_ge, A.mult, ["cs0", "cs1"], ["v2"])
+        for h in range(2):
+            ts(T.alst[:, h:h + 1], T.sec[:, 10 * h + 9:10 * h + 10], T.v2[:, h:h + 1], T.f5[:, h:h + 1], A.mult, A.max,
+               ["sc%d" % h, "v2", "f5"], ["alst0%d" % h])
+
+        def numbers1():
+            for i, (k, keys) in enumerate(((F, ["ab1", "ab2"]), (S, ["sc0", "sc1"]))):
+                ts(T.vi[:, 2 * i:2 * i + 2], k, 1.0 / UNIT, None, A.mult, None, keys, ["vi%d" % i])
+                act(T.sg[:, 2 * i:2 * i + 2], k, AF.Sign, 0.75, -1.0, keys, ["sg%d" % i])
+            act(T.wv[:, :], T.sg[:, :], AF.Identity, 2047.5, 2048.5, ["sg0", "sg1"], ["wv"])
+            ts(T.sv[:, :], T.vi[:, :], 15, None, A.arith_shift_right, None, ["vi0", "vi1"], ["sv"])
+            ts(T.iv[:, :], T.vi[:, :], 511, None, A.bitwise_and, None, ["vi0", "vi1"], ["iv"])
+
+        def numbers2():
+            ts(T.s192[:, :], T.sv[:, :], float(TOK), None, A.mult, None, ["sv"], ["s192"])
+            tt(T.idf[:, :], T.s192[:, :], T.iv[:, :], A.add, ["s192", "iv"], ["idf"])
+
+        def numbers3():
+            for i in range(2):
+                tt(ido[:, i:4:2], T.idf[:, 2 * i:2 * i + 2], T.wv[:, 2 * i:2 * i + 2], A.min, ["idf", "wv"], ["ido%d%d" % (t, i)])
+            for h in range(2):
+                dma("s" if last and h else "y", T.ids[0:1, 64 * t + 32 * h:64 * t + 32 * h + 32], ido[0:16, 2 * h:2 * h + 2],
+                    ["ido%d0" % t, "ido%d1" % t], [], "st")
+
+        def outputs():
+            if t == 0:
+                quant("wq", "ws", 0, 128, "wt", 0, ["wt"], ["wq"])
+                quant("ady", "adys", 0, 128, "cbt", 128, ["cbtz"], ["ady", "adys"])
+            pick("c", "ady", 0, 64, land, 0, 640, "alst", 2, AL + [land], ["ady"])
+            pick("s", "adys", 0, 64, lans, 0, 640, "alst", 2, AL + [lans], ["adys"])
+            mm(6, ("wq", "ws"), 0, ("ady", "adys"), (0,), ["wq", "ady", "adys"])
+            for i in range(2):
+                act(yo[:, i:64:2], ps(6, 32 * i, 32 * i + 32), AF.Copy, 0.0, 1.0, ["ps6"], ["yo%d%d" % (t, i)])
+            dma("y", T.y[:, 64 * t:64 * t + 64], yo[:, :], ["yo%d0" % t, "yo%d1" % t], [], "st")
+        ts(T.alst[:, 4:6], S, 512.0, None, A.mult, None, ["sc0", "sc1"], ["alst2"])
+        if last:
+            numbers1()
+        arrive("ark%d" % t, n_tok, [land, lans])
+        AL = ["alst00", "alst01", "alst1", "alst2", "lz%d" % t]
+        pick("c", "adm", 0, 64, land, 0, 640, "alst", 0, AL + [land], ["adm"])
+        pick("s", "adms", 0, 64, lans, 0, 640, "alst", 0, AL + [lans], ["adms"])
+        for b, ras in ((2, (0,)), (3, (0,)), (0, (0, 32)), (1, (0, 32))):
+            mm(b, EQ, 128 * b, ("adm", "adms"), ras, ["eq", "adm", "adms"])
+        for b in (2, 3):
+            act(T.s4[:, 32 * b:32 * b + 32], ps(b, 32, 64), AF.Copy, 0.0, 1.0, ["ps%d" % b], ["s4%d" % b])
+        ts(T.mv[:, :], F, 1.0, float(G * rank - 128), A.is_ge, A.mult, ["ab1", "ab2"], ["mv"])
+        if last:
+            outputs()
+            numbers2()
+        for h in range(2):
+            ts(T.clst[:, h:h + 1], T.mv[:, h:h + 1], T.gnew[:, h:h + 1], None, A.add, None, ["mv", "gnew%d" % h], ["clst%d" % h])
+        if t == 0:
+            await_("v", writers["nt"])
+
+        def half(b, part, key):
+            tt(T.nt[:, b:128:4], part, T.hc[:, 32 * b:32 * b + 32], A.add, [key, "hc%d" % b], ["nt%d" % b])
+        for b in (2, 3):
+            tt(T.hh[:, 32 * b:32 * b + 32], ps(b, 0, 32), T.s4[:, 32 * b:32 * b + 32], A.add, ["ps%d" % b, "s4%d" % b], ["hh%d" % b])
+        half(0, ps(0, 0, 32), "ps0")
+        half(2, T.hh[:, 64:96], "hh2")
+        half(3, T.hh[:, 96:128], "hh3")
+        half(1, ps(1, 0, 32), "ps1")
+        run("v", lambda e: e.quantize_mx(T[ca][:, 128:256], T[cas][:, 128:256], T.nt[:, :]), ["nt", "nt0", "nt1", "nt2", "nt3"], [ca + "n"])
+        cn, cns = "ca%d" % (t + 1), "cas%d" % (t + 1)
+        CL = ["clst0", "clst1", ca + "n"]
+        pick("c", cn, G * rank, G, ca, 0, 256, "clst", 0, CL + [ca], [cn])
+        pick("s", cns, G * rank, G, cas, 0, 256, "clst", 0, CL + [cas], [cns])
+        if last:
+            dma("y", T.oc[:, :], T[cn][:, own].bitcast(dt.uint8), [cn], [], "st")
+            for k in range(4):
+                dma("y" if k == 3 else "s", T.osc[4 * k:4 * k + 4, :], T[cns][32 * k:32 * k + 4, own], [cns], [], "st")
+            numbers3()
+        else:
+            remote([many(T[cn][:, own].bitcast(dt.uint8), T[cn][:, own].bitcast(dt.uint8), "arc%d" % (t + 1))], [cn])
+            remote([many(T[cns][:, own], T[cns][:, own], "arc%d" % (t + 1))], [cns])
+            quant("xq", "xs", 192 * t + 192, 192 * t + 384, "xt", 768 * t + 768, ["xt%d" % (t + 1)], ["xq%d" % (t + 1)])
+            outputs()
+            numbers1()
+            zero_block(t + 1)
+            numbers2()
+            numbers3()
+            arrive("arc%d" % (t + 1), n_cen, [cn, cns])
+            if t == 0:
+                await_("y", writers["ca1"])
+                dma("y", T.xt[:, 1536:2304], T.x[:, 1536:2304], [], ["xt2"], "ldx2")
+    for k in cnt:
+        if know["p"].get(k, 0) < cnt[k]:
+            g.wait_ge(T.sem[k], cnt[k])

@@ -13,24 +13,24 @@ SCRATCH = {
     "cbt": ("sbuf", [128, 768], "bfloat16"), "xt": ("sbuf", [128, 2304], "bfloat16"), "wt": ("sbuf", [128, 512], "bfloat16"),
     "pt": ("sbuf", [128, 512], "bfloat16"), "zz": ("sbuf", [128, 512], "bfloat16"),
     "ptx": ("sbuf", [128, 512], "bfloat16"), "zzx": ("sbuf", [128, 512], "bfloat16"),
-    "nt": ("sbuf", [128, 512], "bfloat16"), "ct": ("sbuf", [128, 2048], "bfloat16"), "et": ("sbuf", [128, 2048], "bfloat16"),
-    "idf": ("sbuf", [128, 4], "float32"), "ps": ("psum", [128, 4096], "float32"),
+    "nt": ("sbuf", [128, 512], "bfloat16"), "ct": ("sbuf", [128, 2048], "bfloat16"), "et": ("sbuf", [128, 1040], "bfloat16"),
+    "idf": ("sbuf", [128, 4], "float32"), "ps": ("psum", [128, 4096], "float32"), "hc": ("sbuf", [128, 256], "float32"),
 }
 for _c, _s, _n in (("cq", "cqs", 512), ("eq", "eqs", 512), ("cbq", "cbs", 128), ("xq", "xs", 576), ("wq", "ws", 128),
                    ("pq", "pqs", 128), ("zq", "zqs", 128), ("pxq", "pxs", 128), ("zxq", "zxs", 128), ("adm", "adms", 160),
                    ("ady", "adys", 128)):
     SCRATCH[_c] = ("sbuf", [128, _n], CODE)
     SCRATCH[_s] = ("sbuf", [128, _n], "uint8")
-for _b in ("rowi", "k16", "negc", "ma", "mb", "msk", "ls1", "ls2", "dist", "hc", "s4", "hh"):
+for _b in ("rowi", "k16", "negc", "ma", "mb", "msk", "ls1", "ls2", "dist", "hb", "s4", "hh"):
     SCRATCH[_b] = ("sbuf", [128, 128], "float32")
-for _b in ("pcol", "npcol", "qcol", "corr", "ncorr"):
+for _b in ("pcol", "npcol", "qcol", "corr", "ncorr", "q4"):
     SCRATCH[_b] = ("sbuf", [128, 1], "float32")
 for _b in ("dd", "ab", "mx", "sec", "junk"):
     SCRATCH[_b] = ("sbuf", [128, 32], "float32")
 for _b, _n, _d in (("pi", 1, "int32"), ("qi", 1, "int32"), ("ii", 16, "float32"), ("hold", 16, "float32"), ("cut", 16, "float32"),
                    ("flag", 16, "float32"), ("lst", 16, "uint16"), ("cs", 2, "float32"), ("v2", 2, "float32"),
-                   ("f5", 2, "float32"), ("alst", 6, "uint16"), ("mv", 2, "float32"), ("clst", 2, "uint16"),
-                   ("ilst", 2, "uint16"), ("gnew", 2, "float32"), ("vi", 4, "int32"), ("iv", 4, "int32"), ("sv", 4, "int32"),
+                   ("f5", 2, "float32"), ("alst", 6, "uint16"), ("mv", 2, "float32"), ("blst", 8, "uint16"),
+                   ("ilst", 2, "uint16"), ("k8", 8, "float32"), ("vi", 4, "int32"), ("iv", 4, "int32"), ("sv", 4, "int32"),
                    ("s192", 4, "float32"), ("sg", 4, "float32"), ("wv", 4, "float32")):
     SCRATCH[_b] = ("sbuf", [128, _n], _d)
 for _t in range(R):
@@ -42,7 +42,6 @@ for _t in range(R):
     SCRATCH["lans%d" % _t] = ("sbuf", [128, 640], "uint8")
     SCRATCH["yo%d" % _t] = ("sbuf", [128, 64], "float32")
     SCRATCH["ido%d" % _t] = ("sbuf", [128, 4], "float32")
-for _t in range(R + 1):
     SCRATCH["ca%d" % _t] = ("sbuf", [128, 256], CODE)
     SCRATCH["cas%d" % _t] = ("sbuf", [128, 256], "uint8")
 SEMAPHORES = ["qv", "qs", "qt", "qp", "ldcb", "ldx0", "ldx1", "ldx2", "ldw", "st", "sent",
@@ -225,29 +224,31 @@ def rank_program(g, core, T, topo):
     iota(T.pcol[:, :], [[1, 1]], 0, 1, "pcol")
     iota(T.npcol[:, :], [[1, 1]], 0, -1, "npcol")
     iota(T.k16[:, :], [[0, 8], [1, 16]], 0, 0, "k16")
-    fill(T.et[:, :], 0.0, "etz")
     fill(T.cbt[:, 128:768], 0.0, "cbtz")
     ts(T.qi[:, :], T.pi[:, :], 15, None, A.bitwise_and, None, ["pi"], ["qi"])
+    fill(T.et[:, :], 0.0, "etz")
     run("v", lambda e: e.tensor_copy(T.qcol[:, :], T.qi[:, :]), ["qi"], ["qcol"])
-    for h in range(2):
-        ts(T.ilst[:, h:h + 1], T.qcol[:, :], 16.0 * h, None, A.add, None, ["qcol"], ["ilst%d" % h])
     for key, sl, c in (("ct0c", slice(1, 512, 4), 0.0), ("ct0d", slice(3, 512, 4), 0.0), ("ct1a", slice(512, 1024, 4), 1.0),
                        ("ct1b", slice(514, 1024, 4), -1.0)):
         flat(T.ct[:, sl], T.rowi[:, :], c, ["rowi"], key)
 
     quant("cbq", "cbs", 0, 128, "cbt", 0, ["cbt", "cbtz"], ["cbq"])
     own = slice(G * rank, G * rank + G)
+    new = slice(128, 128 + G)
     remote([many(T.cbq[:, 0:G].bitcast(dt.uint8), T.ca0[:, own].bitcast(dt.uint8), "arc0")], ["cbq"])
     remote([many(T.cbs[:, 0:G], T.cas0[:, own], "arc0")], ["cbq"])
+    for h in range(2):
+        ts(T.ilst[:, h:h + 1], T.qcol[:, :], 16.0 * h, None, A.add, None, ["qcol"], ["ilst%d" % h])
+    fill(T.negc[:, :], LOW, "negc")
+    for i, c in enumerate((1.0, 1.0, 0.0, 0.0)):
+        flat(T.ct[:, 1024 + i:1536:4], T.rowi[:, :], c, ["rowi"], "ct2%d" % i)
     pick("c", "ca0", G * rank, G, "cbq", 0, 128, "ilst", 0, ["cbq", "ilst0", "ilst1"], ["ca0"])
     pick("s", "cas0", G * rank, G, "cbs", 0, 128, "ilst", 0, ["cbq", "ilst0", "ilst1"], ["cas0"])
     arrive("arc0", n_cen, ["ca0", "cas0"])
     iota(T.ptx[:, :], [[0, 512]], 0, 0, "ptx")
     iota(T.zzx[:, :], [[0, 512]], 0, 0, "zzx")
     iota(T.hold[:, :], [[0, 4], [1, 4]], 0, 0, "hold")
-    for i, c in enumerate((1.0, 1.0, 0.0, 0.0)):
-        flat(T.ct[:, 1024 + i:1536:4], T.rowi[:, :], c, ["rowi"], "ct2%d" % i)
-    fill(T.negc[:, :], LOW, "negc")
+    iota(T.k8[:, :], [[1, 4], [64, 2]], 0, 0, "k8")
     ts(T.ct[:, 0:512:4], T.rowi[:, :], T.pcol[:, :], None, A.is_ge, None, ["rowi", "pcol"], ["ct0a"])
     ts(T.ct[:, 2:512:4], T.rowi[:, :], T.pcol[:, :], -1.0, A.is_ge, A.mult, ["rowi", "pcol"], ["ct0b"])
     for i, c in enumerate((0.0, -1.0, 1.0, 1.0)):
@@ -260,19 +261,31 @@ def rank_program(g, core, T, topo):
     fill(T.zz[0:64, 1:512:4], 0.0, "zza")
     fill(T.zz[0:64, 3:512:4], 0.0, "zzb")
     fill(T.pt[:, 0:1], 1.0, "pt")
+    quant("xq", "xs", 0, 192, "xt", 0, ["xt0"], ["xq0"])
     fill(T.pt[64:128, 1:2], 1.0, "pt")
     quant("cq", "cqs", 0, 512, "ct", 0, ["ct0a", "ct0b", "ct0c", "ct0d", "ct1a", "ct1b", "ct1c", "ct1d", "ct1e", "ct1f"]
           + ["ct%d%d" % (b, i) for b in (2, 3) for i in range(4)], ["cq"])
     ts(T.msk[:, :], T.k16[:, :], T.qcol[:, :], -33.0 * LIFT, A.is_equal, A.mult, ["k16", "qcol"], ["msk"])
-    ts(T.corr[:, :], T.qcol[:, :], -LIFT, 15.0 * LIFT, A.mult, A.add, ["qcol"], ["corr"])
-    quant("xq", "xs", 0, 192, "xt", 0, ["xt0"], ["xq0"])
-    ts(T.msk[:, :], T.msk[:, :], LIFT, None, A.add, None, [], ["msk"])
-    ts(T.ncorr[:, :], T.corr[:, :], -UNIT, None, A.mult, None, ["corr"], ["ncorr"])
     fill(T.ptx[:, 0:1], 1.0, "ptx")
+    ts(T.corr[:, :], T.qcol[:, :], -LIFT, 15.0 * LIFT, A.mult, A.add, ["qcol"], ["corr"])
+    ts(T.msk[:, :], T.msk[:, :], LIFT, None, A.add, None, [], ["msk"])
     fill(T.ptx[64:128, 1:2], 1.0, "ptx")
+    ts(T.ncorr[:, :], T.corr[:, :], -UNIT, None, A.mult, None, ["corr"], ["ncorr"])
     act(T.dist[:, :], T.rowi[:, :], AF.Abs, T.npcol[:, 0:1], 1.0, ["rowi", "npcol"], ["dist"])
-    for b in range(4):
-        act(T.et[:, 512 * b + b:512 * b + 512:4], T.dist[:, :], AF.Relu, 0.25, -0.25, ["dist", "etz"], ["et%d" % b])
+    for b in range(2):
+        act(T.et[:, 521 * b + 2:521 * b + 514:4], T.dist[:, :], AF.Relu, 0.25, -0.25, ["dist", "etz"], ["et%d" % b])
+    order = [rank] + [s for s in range(N) if s != rank]
+    steps = [-16, 0, 0, 64 * (order[0] - order[1]) + 16, -16, 64 * (order[1] - order[2]) + 16, -16,
+             64 * (order[2] - order[3]) + 16, -16]
+    for i, c in enumerate(steps):
+        flat(T.dd[:, i:20:10], T.rowi[:, 0:2], c / 512, ["rowi"], "dd%d" % i)
+    for h in range(2):
+        act(T.dd[:, 10 * h + 9:10 * h + 10], T.qcol[:, :], AF.Identity, (64.0 * order[3] + 16 + 32 * h) / 512, 1.0 / 512,
+            ["qcol"], ["dq%d" % h])
+    flat(T.ab[:, 0:2], T.rowi[:, 0:2], FAR, ["rowi"], "ab0")
+    act(T.q4[:, :], T.qcol[:, :], AF.Copy, 0.0, 4.0, ["qcol"], ["q4"])
+    for t in range(R):
+        flat(T["lm%d" % t][:, 4:8], T.rowi[:, 0:4], 8.0, ["rowi"], "lp%d" % t)
     await_("y", writers["ca0"])
     dma("y", T.wt[:, :], T.w[:, :], [], ["wt"], "ldw")
     dma("y", T.xt[:, 768:1536], T.x[:, 768:1536], [], ["xt1"], "ldx1")
@@ -282,22 +295,21 @@ def rank_program(g, core, T, topo):
 
     def late_constants():
         flat(T.nt[:, :], T.cbt[:, 128:640], 0.0, ["cbtz"], "nt")
-        for h in range(2):
-            ts(T.gnew[:, h:h + 1], T.qcol[:, :], 128.0 + 16 * h, None, A.add, None, ["qcol"], ["gnew%d" % h])
         quant("adm", "adms", 0, 160, "cbt", 128, ["cbtz"], ["adm", "adms"])
         zero_block(0)
 
     XQ, CQ, EQ = ("xq", "xs"), ("cq", "cqs"), ("eq", "eqs")
+    NT = ["nt0", "nt1", "nt2", "nt3"]
     for t in range(R):
         last = t == R - 1
         ca, cas = "ca%d" % t, "cas%d" % t
         CA = (ca, cas)
         lm, meta, yo, ido = T["lm%d" % t], T["meta%d" % t], T["yo%d" % t], T["ido%d" % t]
         land, lans, snd, sns = "land%d" % t, "lans%d" % t, "snd%d" % t, "sns%d" % t
-        mm(0, XQ, 192 * t, CA, (0,), ["xq%d" % t, ca, cas])
         mm(1, XQ, 192 * t + 64, CA, (0,), ["xq%d" % t, ca, cas])
-        scan(T.ma[:, :], ps(0, 0, 128), T.negc[:, :], LOW, A.max, A.max, ["ps0", "negc"], ["ma"])
+        mm(0, XQ, 192 * t, CA, (0,), ["xq%d" % t, ca, cas])
         scan(T.mb[64:128, :], ps(1, 0, 128, 64), T.negc[64:128, :], LOW, A.max, A.max, ["ps1", "negc"], ["mb"])
+        scan(T.ma[:, :], ps(0, 0, 128), T.negc[:, :], LOW, A.max, A.max, ["ps0", "negc"], ["ma"])
 
         def before(q, out, m, key, p0, k0, k1, step, wr):
             if q == "v":
@@ -313,8 +325,8 @@ def rank_program(g, core, T, topo):
         before("v", T.pt[64:128, 3:512:4], T.mb, "mb", 64, 0, 128, 1, "pt3")
         before("v", T.ptx[64:128, 5:14:4], T.mb, "mb", 64, 31, 96, 32, "px1")
         before("v", T.ptx[64:128, 3:12:4], T.mb, "mb", 64, 31, 96, 32, "px3")
+        before("v", T.ptx[:, 4:13:4], T.ma, "ma", 0, 31, 96, 32, "px0")
         quant("pq", "pqs", 0, 128, "pt", 0, ["pt", "pt0", "pt1", "pt2", "pt3"], ["pq"])
-        before("s", T.ptx[:, 4:13:4], T.ma, "ma", 0, 31, 96, 32, "px0")
         before("s", T.ptx[:, 2:11:4], T.ma, "ma", 0, 31, 96, 32, "px2")
         mm(3, CQ, 128, ("pq", "pqs"), (0,), ["cq", "pq"])
         mm(2, CQ, 0, ("pq", "pqs"), (0,), ["cq", "pq"])
@@ -325,11 +337,14 @@ def rank_program(g, core, T, topo):
             act(T.zz[64:128, el:512:4], ps(3, 0, 128, 64), AF.Relu, c, -1.0, ["ps3"], ["zz%d" % el])
         for el, c in ((0, 1.0), (2, 2.0)):
             ts(T.zz[:, el:512:4], ps(2, 0, 128), c, None, A.is_lt, None, ["ps2"], ["zz%d" % el])
+
+        def below(el, bank, p0):
+            ts(T.zzx[p0:128, el:64:16], ps(bank, 0, 4, p0), CAPP + 1.0, UNIT, A.is_lt, A.mult, ["ps%d" % bank, "zzx"], ["zx%d" % el])
+        below(0, 6, 0)
         quant("zq", "zqs", 0, 128, "zz", 0, ["zza", "zzb", "zz0", "zz1", "zz2", "zz3"], ["zq"])
         mm(4, CQ, 256, ("zq", "zqs"), (0,), ["cq", "zq"])
         mm(5, CQ, 384, ("zq", "zqs"), (0,), ["cq", "zq"])
-        for el, bank, p0 in ((0, 6, 0), (1, 7, 64)):
-            ts(T.zzx[p0:128, el:64:16], ps(bank, 0, 4, p0), CAPP + 1.0, UNIT, A.is_lt, A.mult, ["ps%d" % bank, "zzx"], ["zx%d" % el])
+        below(1, 7, 64)
         quant("zxq", "zxs", 0, 128, "zzx", 0, ["zzx", "zx0", "zx1"], ["zxq"])
         mm(0, CQ, 256, ("zxq", "zxs"), (0,), ["cq", "zxq"])
         for j, ls in ((0, T.ls1), (1, T.ls2)):
@@ -345,6 +360,7 @@ def rank_program(g, core, T, topo):
         mk = "meta%d" % t
         sp0, sp1 = split(rank, 0), split(rank, 1)
         me = slice(64 * rank, 64 * rank + 64)
+        ark = "ark%d" % t
 
         def slots(kind, n):
             d = (oth + [rank])[n]
@@ -356,7 +372,7 @@ def rank_program(g, core, T, topo):
                 pick(kind, o, 64 * rank, 64, x, 192 * t, 192 * t + 192, "lst", 4 * d, LST + ["xq%d" % t], [o])
 
         def send_codes(n):
-            remote([one(oth[n], T[snd][:, 64 * n:64 * n + 64].bitcast(dt.uint8), T[land][:, me].bitcast(dt.uint8), "ark%d" % t, full)],
+            remote([one(oth[n], T[snd][:, 64 * n:64 * n + 64].bitcast(dt.uint8), T[land][:, me].bitcast(dt.uint8), ark, full)],
                    ["%s.%d" % (snd, n)])
 
         def place(d):
@@ -373,33 +389,28 @@ def rank_program(g, core, T, topo):
         remote([one(d, meta[:, 4 * d:4 * d + 4], lm[:, place(d)], "arm%d" % t, sp0[d]) for d in oth], [mk])
         send_codes(1)
         slots("c", 2)
-        remote([one(e, T[sns][:, 64 * m:64 * m + 64], T[lans][:, me], "ark%d" % t, sp1[e]) for m, e in enumerate(oth)],
+        remote([one(e, T[sns][:, 64 * m:64 * m + 64], T[lans][:, me], ark, sp1[e]) for m, e in enumerate(oth)],
                ["%s.%d" % (sns, m) for m in range(3)])
         send_codes(2)
         slots("c", 3)
         if t == 0:
-            quant("eq", "eqs", 0, 512, "et", 0, ["etz"] + ["et%d" % b for b in range(4)], ["eq"])
-            o = [rank] + [s for s in range(N) if s != rank]
-            steps = [-16, 0, 0, 64 * (o[0] - o[1]) + 16, -16, 64 * (o[1] - o[2]) + 16, -16, 64 * (o[2] - o[3]) + 16, -16]
-            fill(T.dd[:, 0:20], -16.0 / 512, "dd")
-            for i, c in enumerate(steps):
-                if c != -16:
-                    run("v", lambda e: e.memset(T.dd[:, i:20:10], c / 512), ["dd"], ["dd%d" % i])
-            for h in range(2):
-                ts(T.dd[:, 10 * h + 9:10 * h + 10], T.qcol[:, :], 64.0 * o[3] + 16 + 32 * h, 1.0 / 512, A.add, A.mult,
-                   ["qcol", "dd"], ["dq%d" % h])
-            fill(T.ab[:, 0:2], FAR, "ab0")
+            for b in range(4):
+                quant("eq", "eqs", 128 * b, 128 * b + 128, "et", 520 * (b % 2) + 2 - 2 * (b // 2), ["etz", "et%d" % (b % 2)],
+                      ["eq%d" % b])
         for b in range(4):
-            mm(4 + b, EQ, 128 * b, CA, (0,), ["eq", ca, cas])
+            mm(4 + b, EQ, 128 * b, CA, (0,), ["eq%d" % b, ca, cas])
+        if t == 0:
+            act(T.hc[:, 128:256], T.cbt[:, 0:128], AF.Copy, 0.0, 1.0, ["cbt"], ["ho"])
+        else:
+            act(T.hc[:, 128:256], T.nt[:, 0:128], AF.Copy, 0.0, 1.0, NT, ["ho"])
         for b in range(4):
-            act(T.hc[:, 32 * b:32 * b + 32], ps(4 + b, G * rank, G * rank + G), AF.Copy, 0.0, 2.0, ["ps%d" % (4 + b)], ["hc%d" % b])
-        fill(lm[:, 4:8], 8.0, "lp%d" % t)
+            act(T.hc[:, b:128:4], ps(4 + b, G * rank, G * rank + G), AF.Copy, 0.0, 2.0, ["ps%d" % (4 + b)], ["hc%d" % b])
         run("v", lambda e: e.tensor_copy(lm[:, 0:4], meta[:, 4 * rank:4 * rank + 4]), [mk], ["lo%d" % t])
         if t == 0:
             late_constants()
         arrive("arm%d" % t, n_meta, ["lm%d" % t])
         LM = ["lm%d" % t, "lo%d" % t, "lp%d" % t]
-        DD = ["dd", "dq0", "dq1"] + ["dd%d" % i for i in (1, 2, 3, 5, 7)]
+        DD = ["dq0", "dq1"] + ["dd%d" % i for i in range(9)]
         for h in range(2):
             scan(T.ab[:, 2 + h:22:2], lm[:, h:20:2], T.dd[:, 10 * h:10 * h + 10], FAR, A.min, A.add, LM + DD, ["ab%d" % (1 + h)])
         for h in range(2):
@@ -407,10 +418,11 @@ def rank_program(g, core, T, topo):
         tt(T.mx[:, 0:20], lm[:, :], T.ab[:, 0:20], A.max, LM + ["ab0", "ab1", "ab2"], ["mx"])
         F, S = T.ab[:, 20:22], T.sec[:, 9:20:10]
         ts(T.f5[:, :], F, 512.0, None, A.mult, None, ["ab1", "ab2"], ["f5"])
+        ts(T.alst[:, 2:4], F, 512.0, None, A.mult, None, ["ab1", "ab2"], ["alst1"])
         for h in range(2):
             scan(T.sec[:, 10 * h:10 * h + 10], T.mx[:, h:20:2], T.dd[:, 10 * h:10 * h + 10], FAR, A.min, A.add, ["mx"] + DD, ["sc%d" % h])
-        ts(T.alst[:, 2:4], F, 512.0, None, A.mult, None, ["ab1", "ab2"], ["alst1"])
         ts(T.v2[:, :], T.cs[:, :], -7.0, 512.0, A.is_ge, A.mult, ["cs0", "cs1"], ["v2"])
+        ts(T.mv[:, :], F, 1.0, 128.0, A.is_ge, A.mult, ["ab1", "ab2"], ["mv"])
         for h in range(2):
             ts(T.alst[:, h:h + 1], T.sec[:, 10 * h + 9:10 * h + 10], T.v2[:, h:h + 1], T.f5[:, h:h + 1], A.mult, A.max,
                ["sc%d" % h, "v2", "f5"], ["alst0%d" % h])
@@ -438,8 +450,8 @@ def rank_program(g, core, T, topo):
             if t == 0:
                 quant("wq", "ws", 0, 128, "wt", 0, ["wt"], ["wq"])
                 quant("ady", "adys", 0, 128, "cbt", 128, ["cbtz"], ["ady", "adys"])
-            pick("c", "ady", 0, 64, land, 0, 640, "alst", 2, AL + [land], ["ady"])
-            pick("s", "adys", 0, 64, lans, 0, 640, "alst", 2, AL + [lans], ["adys"])
+            pick("c", "ady", 0, 64, land, 0, 640, "alst", 2, AL + ["alst2", land], ["ady"])
+            pick("s", "adys", 0, 64, lans, 0, 640, "alst", 2, AL + ["alst2", lans], ["adys"])
             mm(6, ("wq", "ws"), 0, ("ady", "adys"), (0,), ["wq", "ady", "adys"])
             for i in range(2):
                 act(yo[:, i:64:2], ps(6, 32 * i, 32 * i + 32), AF.Copy, 0.0, 1.0, ["ps6"], ["yo%d%d" % (t, i)])
@@ -447,45 +459,46 @@ def rank_program(g, core, T, topo):
         ts(T.alst[:, 4:6], S, 512.0, None, A.mult, None, ["sc0", "sc1"], ["alst2"])
         if last:
             numbers1()
-        arrive("ark%d" % t, n_tok, [land, lans])
-        AL = ["alst00", "alst01", "alst1", "alst2", "lz%d" % t]
+        arrive(ark, n_tok, [land, lans])
+        AL = ["alst00", "alst01", "alst1", "lz%d" % t]
         pick("c", "adm", 0, 64, land, 0, 640, "alst", 0, AL + [land], ["adm"])
         pick("s", "adms", 0, 64, lans, 0, 640, "alst", 0, AL + [lans], ["adms"])
+        for h in range(2):
+            ts(T.blst[:, h:8:2], T.k8[:, h:8:2], T.mv[:, h:h + 1], T.q4[:, 0:1], A.add, A.add, ["k8", "mv", "q4"], ["blst%d" % h])
+        run("v", lambda e: e.tensor_copy(T.hb[:, :], T.hc[:, 0:256].indirect(T.blst[:, 0:8])),
+            ["blst0", "blst1", "ho", "hc0", "hc1", "hc2", "hc3"], ["hb"])
         for b, ras in ((2, (0,)), (3, (0,)), (0, (0, 32)), (1, (0, 32))):
-            mm(b, EQ, 128 * b, ("adm", "adms"), ras, ["eq", "adm", "adms"])
+            mm(b, EQ, 128 * b, ("adm", "adms"), ras, ["eq%d" % b, "adm", "adms"])
         for b in (2, 3):
             act(T.s4[:, 32 * b:32 * b + 32], ps(b, 32, 64), AF.Copy, 0.0, 1.0, ["ps%d" % b], ["s4%d" % b])
-        ts(T.mv[:, :], F, 1.0, float(G * rank - 128), A.is_ge, A.mult, ["ab1", "ab2"], ["mv"])
         if last:
             outputs()
             numbers2()
-        for h in range(2):
-            ts(T.clst[:, h:h + 1], T.mv[:, h:h + 1], T.gnew[:, h:h + 1], None, A.add, None, ["mv", "gnew%d" % h], ["clst%d" % h])
         if t == 0:
             await_("v", writers["nt"])
 
         def half(b, part, key):
-            tt(T.nt[:, b:128:4], part, T.hc[:, 32 * b:32 * b + 32], A.add, [key, "hc%d" % b], ["nt%d" % b])
+            tt(T.nt[:, b:128:4], part, T.hb[:, 32 * b:32 * b + 32], A.add, [key, "hb"], ["nt%d" % b])
         for b in (2, 3):
             tt(T.hh[:, 32 * b:32 * b + 32], ps(b, 0, 32), T.s4[:, 32 * b:32 * b + 32], A.add, ["ps%d" % b, "s4%d" % b], ["hh%d" % b])
         half(0, ps(0, 0, 32), "ps0")
         half(2, T.hh[:, 64:96], "hh2")
         half(3, T.hh[:, 96:128], "hh3")
         half(1, ps(1, 0, 32), "ps1")
-        run("v", lambda e: e.quantize_mx(T[ca][:, 128:256], T[cas][:, 128:256], T.nt[:, :]), ["nt", "nt0", "nt1", "nt2", "nt3"], [ca + "n"])
-        cn, cns = "ca%d" % (t + 1), "cas%d" % (t + 1)
-        CL = ["clst0", "clst1", ca + "n"]
-        pick("c", cn, G * rank, G, ca, 0, 256, "clst", 0, CL + [ca], [cn])
-        pick("s", cns, G * rank, G, cas, 0, 256, "clst", 0, CL + [cas], [cns])
+        nk = ca + "n"
+        run("v", lambda e: e.quantize_mx(T[ca][:, 128:256], T[cas][:, 128:256], T.nt[:, :]), ["nt"] + NT, [nk])
         if last:
-            dma("y", T.oc[:, :], T[cn][:, own].bitcast(dt.uint8), [cn], [], "st")
+            dma("y", T.oc[:, :], T[ca][:, new].bitcast(dt.uint8), [nk], [], "st")
             for k in range(4):
-                dma("y" if k == 3 else "s", T.osc[4 * k:4 * k + 4, :], T[cns][32 * k:32 * k + 4, own], [cns], [], "st")
+                dma("y" if k == 3 else "s", T.osc[4 * k:4 * k + 4, :], T[cas][32 * k:32 * k + 4, new], [nk], [], "st")
             numbers3()
         else:
-            remote([many(T[cn][:, own].bitcast(dt.uint8), T[cn][:, own].bitcast(dt.uint8), "arc%d" % (t + 1))], [cn])
-            remote([many(T[cns][:, own], T[cns][:, own], "arc%d" % (t + 1))], [cns])
+            cn, cns = "ca%d" % (t + 1), "cas%d" % (t + 1)
+            remote([many(T[ca][:, new].bitcast(dt.uint8), T[cn][:, own].bitcast(dt.uint8), "arc%d" % (t + 1))], [nk])
+            remote([many(T[cas][:, new], T[cns][:, own], "arc%d" % (t + 1))], [nk])
             quant("xq", "xs", 192 * t + 192, 192 * t + 384, "xt", 768 * t + 768, ["xt%d" % (t + 1)], ["xq%d" % (t + 1)])
+            pick("c", cn, G * rank, G, ca, 128, 256, "ilst", 0, [nk, "ilst0", "ilst1"], [cn])
+            pick("s", cns, G * rank, G, cas, 128, 256, "ilst", 0, [nk, "ilst0", "ilst1"], [cns])
             outputs()
             numbers1()
             zero_block(t + 1)

@@ -3,48 +3,54 @@ from concourse.mybir import dt, AluOpType as A, ActivationFunctionType as AF
 
 CODE = "float8_e4m3fn_x4"
 N, G, TOK, R, CAPP = 4, 32, 192, 3, 64
-UNIT = 2.0 ** -18
+UNIT = 2.0 ** -20
 WIN = 512
 FAR = 64.0
 LOW = -1.0e29
-LIFT = 1024.0
+LIFT = 256.0
+W = 136
+PAD = 8.0
+BIG = 1024.0
+ONE, TWO = (CAPP + 0.5) / 128, 1.5
+PRE = 1
 
 SCRATCH = {
     "cbt": ("sbuf", [128, 768], "bfloat16"), "xt": ("sbuf", [128, 2304], "bfloat16"), "wt": ("sbuf", [128, 512], "bfloat16"),
-    "pt": ("sbuf", [128, 512], "bfloat16"), "zz": ("sbuf", [128, 512], "bfloat16"),
-    "ptx": ("sbuf", [128, 512], "bfloat16"), "zzx": ("sbuf", [128, 512], "bfloat16"),
+    "pt": ("sbuf", [128, 4 * W], "bfloat16"), "zz": ("sbuf", [128, 4 * W], "bfloat16"),
     "nt": ("sbuf", [128, 512], "bfloat16"), "ct": ("sbuf", [128, 2048], "bfloat16"), "et": ("sbuf", [128, 1040], "bfloat16"),
-    "idf": ("sbuf", [128, 4], "float32"), "ps": ("psum", [128, 4096], "float32"), "hc": ("sbuf", [128, 256], "float32"),
+    "ps": ("psum", [128, 4096], "float32"), "hc": ("sbuf", [128, 384], "float32"), "ls": ("sbuf", [128, 2 * W], "float32"),
+    "msk": ("sbuf", [128, W], "float32"), "ab": ("sbuf", [128, 80], "float32"), "lm": ("sbuf", [128, 24 * R], "bfloat16"),
 }
 for _c, _s, _n in (("cq", "cqs", 512), ("eq", "eqs", 512), ("cbq", "cbs", 128), ("xq", "xs", 576), ("wq", "ws", 128),
-                   ("pq", "pqs", 128), ("zq", "zqs", 128), ("pxq", "pxs", 128), ("zxq", "zxs", 128), ("adm", "adms", 160),
-                   ("ady", "adys", 128)):
+                   ("pq", "pqs", W), ("zq", "zqs", W), ("adm", "adms", 160), ("ady", "adys", 128)):
     SCRATCH[_c] = ("sbuf", [128, _n], CODE)
     SCRATCH[_s] = ("sbuf", [128, _n], "uint8")
-for _b in ("rowi", "k16", "negc", "ma", "mb", "msk", "ls1", "ls2", "dist", "hb", "s4", "hh"):
+for _b in ("rowi", "k16", "mk1", "ma", "mb", "dist", "hb"):
     SCRATCH[_b] = ("sbuf", [128, 128], "float32")
-for _b in ("pcol", "npcol", "qcol", "corr", "ncorr", "q4"):
+for _b in ("pcol", "lo5", "hi5", "thr", "npcol", "qcol", "q1", "b0", "b1", "corr", "ncorr", "q4"):
     SCRATCH[_b] = ("sbuf", [128, 1], "float32")
-for _b in ("dd", "ab", "mx", "sec", "junk"):
-    SCRATCH[_b] = ("sbuf", [128, 32], "float32")
-for _b, _n, _d in (("pi", 1, "int32"), ("qi", 1, "int32"), ("ii", 16, "float32"), ("hold", 16, "float32"), ("cut", 16, "float32"),
-                   ("flag", 16, "float32"), ("lst", 16, "uint16"), ("cs", 2, "float32"), ("v2", 2, "float32"),
-                   ("f5", 2, "float32"), ("alst", 6, "uint16"), ("mv", 2, "float32"), ("blst", 8, "uint16"),
-                   ("ilst", 2, "uint16"), ("k8", 8, "float32"), ("vi", 4, "int32"), ("iv", 4, "int32"), ("sv", 4, "int32"),
-                   ("s192", 4, "float32"), ("sg", 4, "float32"), ("wv", 4, "float32")):
+for _b in ("dd", "de", "mx", "cn", "cc"):
+    SCRATCH[_b] = ("sbuf", [128, 40], "float32")
+for _b in ("v2", "f5", "mv", "ug", "uf", "um"):
+    SCRATCH[_b] = ("sbuf", [128, 2], "float32")
+for _b in ("sg", "wv", "pf", "pg", "z1", "z4"):
+    SCRATCH[_b] = ("sbuf", [128, 4], "float32")
+for _b, _n, _d in (("pi", 1, "int32"), ("qi", 1, "int32"), ("ii", 16, "float32"), ("flag", 16, "float32"), ("lst", 16, "uint16"),
+                   ("alst", 6, "uint16"), ("blst", 8, "uint16"), ("ilst", 2, "uint16"), ("k8", 8, "float32"),
+                   ("vi", 4, "int32"), ("iv", 4, "int32"), ("col", 4, "int32"), ("ur", 2, "int32"), ("pv", 2, "uint16"),
+                   ("pk", 2, "uint16")):
     SCRATCH[_b] = ("sbuf", [128, _n], _d)
 for _t in range(R):
     SCRATCH["meta%d" % _t] = ("sbuf", [128, 16], "bfloat16")
-    SCRATCH["lm%d" % _t] = ("sbuf", [128, 20], "bfloat16")
     SCRATCH["snd%d" % _t] = ("sbuf", [128, 192], CODE)
     SCRATCH["sns%d" % _t] = ("sbuf", [128, 192], "uint8")
-    SCRATCH["land%d" % _t] = ("sbuf", [128, 640], CODE)
-    SCRATCH["lans%d" % _t] = ("sbuf", [128, 640], "uint8")
+    SCRATCH["land%d" % _t] = ("sbuf", [128, 768], CODE)
+    SCRATCH["lans%d" % _t] = ("sbuf", [128, 768], "uint8")
     SCRATCH["yo%d" % _t] = ("sbuf", [128, 64], "float32")
     SCRATCH["ido%d" % _t] = ("sbuf", [128, 4], "float32")
     SCRATCH["ca%d" % _t] = ("sbuf", [128, 256], CODE)
     SCRATCH["cas%d" % _t] = ("sbuf", [128, 256], "uint8")
-SEMAPHORES = ["qv", "qs", "qt", "qp", "ldcb", "ldx0", "ldx1", "ldx2", "ldw", "st", "sent",
+SEMAPHORES = ["qv", "qs", "qt", "qp", "ldcb", "ldx0", "ldx1", "ldx2", "ldw", "st", "sent", "left", "arf",
               "arc0", "arc1", "arc2", "arm0", "arm1", "arm2", "ark0", "ark1", "ark2"]
 
 
@@ -57,7 +63,7 @@ def rank_program(g, core, T, topo):
     def others(r):
         def hops(d):
             a, b = topo.chip(cores[r]), topo.chip(cores[d])
-            return 0 if a == b else (1 if topo.mates(a, b) or topo.same_plane(a, b) else 2)
+            return 1 if topo.mates(a, b) or topo.same_plane(a, b) else 2
         return sorted([d for d in range(N) if d != r], key=lambda d: -hops(d))
 
     def bits(es):
@@ -72,23 +78,25 @@ def rank_program(g, core, T, topo):
             es = [e for e in es if e in topo.engines(cores[r], cores[d])]
         return es
 
-    def split(r, kind):
-        es = common(r)
-        h, q = len(es) // 2, len(es) // 4
-        a, b, c = others(r)
-        if kind == 0:
-            return {a: es[:h], b: es[h:h + q], c: es[h + q:]}
-        return {a: es[h:], b: es[:q], c: es[q:h]}
-
     oth = others(rank)
+    far = oth[0]
     full = common(rank)
     dst = {}
     for d in oth:
         rid, pid, _ = topo.addr(cores[d])
         dst[d] = (rid, pid)
-    n_meta = sum(len(split(s, 0)[rank]) for s in range(N) if s != rank)
-    n_tok = sum(len(split(s, 1)[rank]) + len(common(s)) for s in range(N) if s != rank)
-    n_cen = sum(2 * len(common(s)) for s in range(N) if s != rank)
+    n_meta = sum(len(common(s)) for s in range(N) if s != rank)
+    n_tok = 2 * n_meta
+    n_cen = 2 * n_meta
+
+    def senders(d, t):
+        return sorted(others(d)[1:]) + others(d)[:1] if t == PRE else sorted(others(d))
+
+    def column(d, s, t):
+        return 64 * s + (TOK - 64 if t == PRE and s > others(d)[0] else 0)
+
+    def keys_at(t):
+        return [column(rank, s, t) / 512 + (s - (t == PRE and s > far)) * TOK * UNIT for s in [rank] + senders(rank, t)]
 
     ENG = {"v": g.vector, "s": g.scalar, "t": g.tensor, "p": g, "y": g.sync}
     cnt = {}
@@ -151,18 +159,12 @@ def rank_program(g, core, T, topo):
         for k in keys:
             writers.setdefault(k, []).append(rec)
 
-    def remote(transfers, rd):
+    def remote(ds, src, to, sem, rd, left="sent"):
         await_("p", deps("p", rd, []))
-        g.remote_dma_fused([t for t, _ in transfers], local_sem=T.sem["sent"])
-        cnt["sent"] = cnt.get("sent", 0) + sum(n for _, n in transfers)
-
-    def one(d, src, to, sem, es):
-        return (RemoteDMATransfer(dst_ids=[DstId(rid=dst[d][0], pnc=dst[d][1])], dma_engine_mask=bits(es),
-                                  remote_sem=T.sem[sem], src=src, dst=to), len(es))
-
-    def many(src, to, sem):
-        return (RemoteDMATransfer(dst_ids=[DstId(rid=dst[d][0], pnc=dst[d][1]) for d in oth], dma_engine_mask=bits(full),
-                                  remote_sem=T.sem[sem], srcs=[src], dsts=[to for d in oth]), len(full))
+        g.remote_dma_fused([RemoteDMATransfer(dst_ids=[DstId(rid=dst[d][0], pnc=dst[d][1]) for d in ds],
+                                              dma_engine_mask=bits(full), remote_sem=T.sem[sem],
+                                              srcs=[src], dsts=[to for d in ds])], local_sem=T.sem[left])
+        cnt[left] = cnt.get(left, 0) + len(full)
 
     def ts(out, in0, s1, s2, o0, o1, rd, wr):
         if o1 is None:
@@ -176,8 +178,8 @@ def rank_program(g, core, T, topo):
     def scan(out, a, b, first, o0, o1, rd, wr):
         run("v", lambda e: e.tensor_tensor_scan(out, a, b, first, o0, o1), rd, wr)
 
-    def act(out, in_, func, bias, scale, rd, wr, total=None):
-        run("s", lambda e: e.activation(out, in_, func, bias=bias, scale=scale, accum_out=total), rd, wr)
+    def act(out, in_, func, bias, scale, rd, wr):
+        run("s", lambda e: e.activation(out, in_, func, bias=bias, scale=scale), rd, wr)
 
     def fill(ap, c, key):
         run("v", lambda e: e.memset(ap, c), [], [key])
@@ -188,14 +190,12 @@ def rank_program(g, core, T, topo):
     def quant(c, s, a, b, tile, x, keys, out):
         run("v", lambda e: e.quantize_mx(T[c][:, a:b], T[s][:, a:b], T[tile][:, x:x + 4 * (b - a)]), keys, out)
 
-    def mm(bank, l, la, r, ras, rd):
+    def mm(bank, l, la, r, ra, rd, n=128, part=None):
         lc, lsc = l
         rc, rs = r
-        await_("t", deps("t", rd, ["ps%d" % bank]))
-        for i, ra in enumerate(ras):
-            call = g.tensor.matmul_mx(T.ps[:, 512 * bank:512 * bank + 128], T[lc][:, la:la + 128], T[lsc][:, la:la + 128],
-                                      T[rc][:, ra:ra + 128], T[rs][:, ra:ra + 128], i == 0, i == len(ras) - 1)
-        call.then_inc(T.sem["qt"], 1)
+        await_("t", deps("t", rd, [] if part == 0 else ["ps%d" % bank]))
+        g.tensor.matmul_mx(T.ps[:, 512 * bank:512 * bank + n], T[lc][:, la:la + 128], T[lsc][:, la:la + 128],
+                           T[rc][:, ra:ra + n], T[rs][:, ra:ra + n], part != 0, part != 1).then_inc(T.sem["qt"], 1)
         note(record("t", "qt", 1), rd, ["ps%d" % bank])
 
     def pick(kind, dstb, da, n, srcb, sa, sb, lstb, la, rd, wr):
@@ -222,144 +222,197 @@ def rank_program(g, core, T, topo):
     iota(T.pi[:, :], [[1, 1]], 0, 1, "pi", False)
     iota(T.rowi[:, :], [[1, 128]], 0, 0, "rowi")
     iota(T.pcol[:, :], [[1, 1]], 0, 1, "pcol")
-    iota(T.npcol[:, :], [[1, 1]], 0, -1, "npcol")
-    iota(T.k16[:, :], [[0, 8], [1, 16]], 0, 0, "k16")
     fill(T.cbt[:, 128:768], 0.0, "cbtz")
+    fill(T.lm[:, :], PAD, "lp")
     ts(T.qi[:, :], T.pi[:, :], 15, None, A.bitwise_and, None, ["pi"], ["qi"])
-    fill(T.et[:, :], 0.0, "etz")
+    fill(T.ct[:, 1:512:2], 0.0, "ct0c")
+    fill(T.ct[0:64, 513:1024:2], 0.0, "ct1e")
     run("v", lambda e: e.tensor_copy(T.qcol[:, :], T.qi[:, :]), ["qi"], ["qcol"])
-    for key, sl, c in (("ct0c", slice(1, 512, 4), 0.0), ("ct0d", slice(3, 512, 4), 0.0), ("ct1a", slice(512, 1024, 4), 1.0),
-                       ("ct1b", slice(514, 1024, 4), -1.0)):
-        flat(T.ct[:, sl], T.rowi[:, :], c, ["rowi"], key)
+    fill(T.pt[0:64, 1:512:2], 0.0, "pt")
+    fill(T.zz[:, 3:4 * W:4], 0.0, "zza")
+    flat(T.ct[:, 512:1024:4], T.rowi[:, :], 1.0, ["rowi"], "ct1a")
+    flat(T.ct[:, 514:1024:4], T.rowi[:, :], -1.0, ["rowi"], "ct1b")
+    for i, c in ((0, 1.0), (2, 0.0), (3, 0.0)):
+        flat(T.ct[:, 1024 + i:1536:4], T.rowi[:, :], c, ["rowi"], "ct2%d" % i)
 
-    quant("cbq", "cbs", 0, 128, "cbt", 0, ["cbt", "cbtz"], ["cbq"])
+    quant("cbq", "cbs", 0, 128, "cbt", 0, ["cbt", "cbtz", "lp"], ["cbq"])
     own = slice(G * rank, G * rank + G)
     new = slice(128, 128 + G)
-    remote([many(T.cbq[:, 0:G].bitcast(dt.uint8), T.ca0[:, own].bitcast(dt.uint8), "arc0")], ["cbq"])
-    remote([many(T.cbs[:, 0:G], T.cas0[:, own], "arc0")], ["cbq"])
+
+    def send_centroids(c, s, cols, t, key):
+        remote(oth, T[c][:, cols].bitcast(dt.uint8), T["ca%d" % t][:, own].bitcast(dt.uint8), "arc%d" % t, [key])
+        remote(oth, T[s][:, cols], T["cas%d" % t][:, own], "arc%d" % t, [key])
+    send_centroids("cbq", "cbs", slice(0, G), 0, "cbq")
     for h in range(2):
         ts(T.ilst[:, h:h + 1], T.qcol[:, :], 16.0 * h, None, A.add, None, ["qcol"], ["ilst%d" % h])
-    fill(T.negc[:, :], LOW, "negc")
-    for i, c in enumerate((1.0, 1.0, 0.0, 0.0)):
-        flat(T.ct[:, 1024 + i:1536:4], T.rowi[:, :], c, ["rowi"], "ct2%d" % i)
+    ts(T.lo5[:, :], T.pcol[:, :], 64.0, 0.5, A.is_lt, A.mult, ["pcol"], ["lo5"])
+    ts(T.hi5[:, :], T.pcol[:, :], 64.0, 0.5, A.is_ge, A.mult, ["pcol"], ["hi5"])
+    fill(T.pt[:, 512:4 * W], 0.0, "ptr")
     pick("c", "ca0", G * rank, G, "cbq", 0, 128, "ilst", 0, ["cbq", "ilst0", "ilst1"], ["ca0"])
     pick("s", "cas0", G * rank, G, "cbs", 0, 128, "ilst", 0, ["cbq", "ilst0", "ilst1"], ["cas0"])
     arrive("arc0", n_cen, ["ca0", "cas0"])
-    iota(T.ptx[:, :], [[0, 512]], 0, 0, "ptx")
-    iota(T.zzx[:, :], [[0, 512]], 0, 0, "zzx")
-    iota(T.hold[:, :], [[0, 4], [1, 4]], 0, 0, "hold")
-    iota(T.k8[:, :], [[1, 4], [64, 2]], 0, 0, "k8")
+    iota(T.k16[:, :], [[0, 8], [1, 16]], 0, 0, "k16")
+    iota(T.et[:, :], [[0, 1040]], 0, 0, "etz")
+    iota(T.k8[:, :], [[3, 4], [192, 2]], 1, 0, "k8")
+    ts(T.npcol[:, :], T.pcol[:, :], -1.0, None, A.mult, None, ["pcol"], ["npcol"])
+    flat(T.ct[:, 1025:1536:4], T.rowi[:, :], T.lo5[:, 0:1], ["rowi", "lo5"], "ct21")
+    for i, c in enumerate((0.0, T.hi5[:, 0:1], 1.0, 0.0)):
+        flat(T.ct[:, 1536 + i:2048:4], T.rowi[:, :], c, ["rowi", "hi5"], "ct3%d" % i)
+    act(T.q1[:, :], T.qcol[:, :], AF.Identity, 1.0, 1.0, ["qcol"], ["q1"])
+    act(T.thr[:, :], T.hi5[:, :], AF.Identity, ONE, 2 * (TWO - ONE), ["hi5"], ["thr"])
     ts(T.ct[:, 0:512:4], T.rowi[:, :], T.pcol[:, :], None, A.is_ge, None, ["rowi", "pcol"], ["ct0a"])
     ts(T.ct[:, 2:512:4], T.rowi[:, :], T.pcol[:, :], -1.0, A.is_ge, A.mult, ["rowi", "pcol"], ["ct0b"])
-    for i, c in enumerate((0.0, -1.0, 1.0, 1.0)):
-        fill(T.ct[:, 1536 + i:2048:4], c, "ct3%d" % i)
-    ts(T.ct[64:128, 513:1024:4], T.rowi[64:128, :], T.pcol[64:128, :], None, A.is_ge, None, ["rowi", "pcol"], ["ct1c"])
-    ts(T.ct[64:128, 515:1024:4], T.rowi[64:128, :], T.pcol[64:128, :], -1.0, A.is_ge, A.mult, ["rowi", "pcol"], ["ct1d"])
-    fill(T.ct[0:64, 513:1024:4], 0.0, "ct1e")
-    fill(T.ct[0:64, 515:1024:4], 0.0, "ct1f")
-    fill(T.pt[:, :], 0.0, "pt")
-    fill(T.zz[0:64, 1:512:4], 0.0, "zza")
-    fill(T.zz[0:64, 3:512:4], 0.0, "zzb")
-    fill(T.pt[:, 0:1], 1.0, "pt")
+    for u in range(2):
+        for el, c in ((1, 1.0), (3, -1.0)):
+            ts(T.ct[64:128, 512 + 256 * u + el:768 + 256 * u:4], T.rowi[64:128, 64:128], T.pcol[64:128, :], c, A.is_ge, A.mult,
+               ["rowi", "pcol"], ["ct1%d%d" % (u, el)])
+    fill(T.pt[:, 0:1], 1.0, "pt0c")
+    fill(T.pt[64:128, 1:2], 1.0, "pt1c")
+    await_("v", writers["ptr"])
+    fill(T.pt[:, 516:4 * W:8], 1.0, "pt2c")
+    fill(T.pt[:, 512:513], 1.0 / 128, "pt3c")
+    fill(T.pt[64:128, 513:514], 1.0 / 128, "pt4c")
     quant("xq", "xs", 0, 192, "xt", 0, ["xt0"], ["xq0"])
-    fill(T.pt[64:128, 1:2], 1.0, "pt")
-    quant("cq", "cqs", 0, 512, "ct", 0, ["ct0a", "ct0b", "ct0c", "ct0d", "ct1a", "ct1b", "ct1c", "ct1d", "ct1e", "ct1f"]
+    ts(T.ct[0:1, 1027:1536:4], T.k16[0:1, :], 15.0, None, A.is_lt, None, ["k16"], ["ct23"])
+    fill(T.zz[0:1, 515:4 * W:8], LIFT, "zza")
+    fill(T.zz[32:33, 3:4 * W:4], 32.0, "zzb")
+    await_("v", writers["ct33"])
+    fill(T.ct[32:33, 1027:2048:4], 1.0, "ct4")
+    ts(T.msk[:, 0:128], T.k16[:, :], T.qcol[:, :], -16.0 * LIFT, A.is_equal, A.mult, ["k16", "qcol"], ["msk"])
+    quant("cq", "cqs", 0, 512, "ct", 0, ["ct0a", "ct0b", "ct0c", "ct1a", "ct1b", "ct101", "ct103", "ct111", "ct113", "ct1e", "ct4"]
           + ["ct%d%d" % (b, i) for b in (2, 3) for i in range(4)], ["cq"])
-    ts(T.msk[:, :], T.k16[:, :], T.qcol[:, :], -33.0 * LIFT, A.is_equal, A.mult, ["k16", "qcol"], ["msk"])
-    fill(T.ptx[:, 0:1], 1.0, "ptx")
-    ts(T.corr[:, :], T.qcol[:, :], -LIFT, 15.0 * LIFT, A.mult, A.add, ["qcol"], ["corr"])
-    ts(T.msk[:, :], T.msk[:, :], LIFT, None, A.add, None, [], ["msk"])
-    fill(T.ptx[64:128, 1:2], 1.0, "ptx")
-    ts(T.ncorr[:, :], T.corr[:, :], -UNIT, None, A.mult, None, ["corr"], ["ncorr"])
+    ts(T.mk1[:, :], T.k16[:, :], T.q1[:, :], LIFT, A.is_equal, A.mult, ["k16", "q1"], ["mk1"])
+    ts(T.corr[:, :], T.qcol[:, :], 15.0, LIFT, A.is_lt, A.mult, ["qcol"], ["corr"])
+    fill(T.msk[:, 128:W:2], -16.0 * LIFT, "mska")
+    fill(T.msk[:, 129:W:2], 0.0, "mskb")
+    tt(T.msk[:, 0:128], T.msk[:, 0:128], T.mk1[:, :], A.add, ["mk1"], ["msk"])
+    fill(T.nt[:, 128:512], 0.0, "nt")
+    quant("adm", "adms", 0, 160, "cbt", 128, ["cbtz"], ["adm", "adms"])
+    quant("ady", "adys", 0, 128, "cbt", 128, ["cbtz"], ["ady", "adys"])
+    at = keys_at(0)
+    for key, sl, c in (("dd0", slice(0, 40, 4), -16.0 / 512), ("dd1", slice(1, 40, 4), -2.0), ("dd2", slice(2, 40, 4), 0.0),
+                       ("dd3", slice(3, 40, 20), 2.0 + 16.0 / 512), ("dd4", slice(7, 40, 20), 2.0 + 16.0 / 512 + at[0] - at[1]),
+                       ("dd5", slice(11, 40, 20), 2.0 + 16.0 / 512 + at[1] - at[2]),
+                       ("dd6", slice(15, 40, 20), 2.0 + 16.0 / 512 + at[2] - at[3])):
+        flat(T.dd[:, sl], T.rowi[:, 0:len(range(40)[sl])], c, ["rowi"], key)
+    flat(T.cc[:, 0:18:2], T.rowi[:, 0:9], 1.0, ["rowi"], "cc0")
+    flat(T.cc[:, 1:14:4], T.rowi[:, 0:4], BIG, ["rowi"], "cc1")
+    for h in range(2):
+        act(T.dd[:, 20 * h + 17:20 * h + 18], T.qcol[:, :], AF.Identity, at[3] + (16.0 + 32 * h) / 512, 1.0 / 512,
+            ["qcol", "dd1"], ["dq%d" % h])
+    act(T.ncorr[:, :], T.corr[:, :], AF.Copy, 0.0, -UNIT, ["corr"], ["ncorr"])
     act(T.dist[:, :], T.rowi[:, :], AF.Abs, T.npcol[:, 0:1], 1.0, ["rowi", "npcol"], ["dist"])
     for b in range(2):
         act(T.et[:, 521 * b + 2:521 * b + 514:4], T.dist[:, :], AF.Relu, 0.25, -0.25, ["dist", "etz"], ["et%d" % b])
-    order = [rank] + [s for s in range(N) if s != rank]
-    steps = [-16, 0, 0, 64 * (order[0] - order[1]) + 16, -16, 64 * (order[1] - order[2]) + 16, -16,
-             64 * (order[2] - order[3]) + 16, -16]
-    for i, c in enumerate(steps):
-        flat(T.dd[:, i:20:10], T.rowi[:, 0:2], c / 512, ["rowi"], "dd%d" % i)
-    for h in range(2):
-        act(T.dd[:, 10 * h + 9:10 * h + 10], T.qcol[:, :], AF.Identity, (64.0 * order[3] + 16 + 32 * h) / 512, 1.0 / 512,
-            ["qcol"], ["dq%d" % h])
-    flat(T.ab[:, 0:2], T.rowi[:, 0:2], FAR, ["rowi"], "ab0")
-    act(T.q4[:, :], T.qcol[:, :], AF.Copy, 0.0, 4.0, ["qcol"], ["q4"])
-    for t in range(R):
-        flat(T["lm%d" % t][:, 4:8], T.rowi[:, 0:4], 8.0, ["rowi"], "lp%d" % t)
     await_("y", writers["ca0"])
     dma("y", T.wt[:, :], T.w[:, :], [], ["wt"], "ldw")
     dma("y", T.xt[:, 768:1536], T.x[:, 768:1536], [], ["xt1"], "ldx1")
+    STEPS = ["dq0", "dq1"] + ["dd%d" % i for i in range(7)]
 
-    def zero_block(t):
-        quant("land%d" % t, "lans%d" % t, WIN, WIN + 128, "cbt", 128, ["cbtz"], ["lz%d" % t])
+    def zero_block(t, i):
+        quant("land%d" % t, "lans%d" % t, WIN + 128 * i, WIN + 128 * i + 128, "cbt", 128, ["cbtz"], ["lz%d%d" % (t, i)])
 
-    def late_constants():
-        flat(T.nt[:, :], T.cbt[:, 128:640], 0.0, ["cbtz"], "nt")
-        quant("adm", "adms", 0, 160, "cbt", 128, ["cbtz"], ["adm", "adms"])
-        zero_block(0)
+    def gap_constants(step):
+        if step == 0:
+            flat(T.cc[:, 3:16:4], T.rowi[:, 0:4], 1.0 / BIG, ["rowi"], "cc2")
+            flat(T.cc[:, 17:18], T.rowi[:, 0:1], 1.0, ["rowi"], "cc3")
+        else:
+            flat(T.ab[:, 0:4], T.rowi[:, 0:4], FAR, ["rowi"], "ab")
+            act(T.q4[:, :], T.qcol[:, :], AF.Copy, 0.0, 12.0, ["qcol"], ["q4"])
+        for b in (2 * step, 2 * step + 1):
+            quant("eq", "eqs", 128 * b, 128 * b + 128, "et", 520 * (b % 2) + 2 - 2 * (b // 2), ["etz", "et%d" % (b % 2)], ["eq%d" % b])
 
+    def whole_constants(step):
+        a = keys_at(PRE)
+        if step == 0:
+            for h in range(2):
+                act(T.de[:, 20 * h:20 * h + 15], T.dd[:, 20 * h:20 * h + 15], AF.Copy, 0.0, 1.0, STEPS, ["de%d" % h])
+            act(T.b0[:, :], T.corr[:, :], AF.Identity, 160.0, -257.0, ["corr"], ["b0"])
+            act(T.b1[:, :], T.corr[:, :], AF.Identity, float(TOK), 1.0, ["corr"], ["b1"])
+            return
+        for h in range(2):
+            act(T.de[:, 20 * h + 15:20 * h + 16], T.qcol[:, :], AF.Identity, 2.0 + a[2] - a[3] + (32 * h - 80.0) / 512, 1.0 / 512,
+                ["qcol"], ["de%d" % (2 + h)])
+        for i, (x, c) in enumerate(((16, 97.0 / 512), (17, a[3] - 1.0 / 512), (7, 2.0 + 16.0 / 512 + a[0] - a[1]),
+                                    (11, 2.0 + 16.0 / 512 + a[1] - a[2]))):
+            flat(T.de[:, x:40:20], T.rowi[:, 0:2], c, ["rowi"] + (["de0", "de1"] if x < 15 else []), "de%d" % (4 + i))
+
+    zero_block(0, 0)
     XQ, CQ, EQ = ("xq", "xs"), ("cq", "cqs"), ("eq", "eqs")
     NT = ["nt0", "nt1", "nt2", "nt3"]
     for t in range(R):
         last = t == R - 1
+        pre = t == PRE
         ca, cas = "ca%d" % t, "cas%d" % t
         CA = (ca, cas)
-        lm, meta, yo, ido = T["lm%d" % t], T["meta%d" % t], T["yo%d" % t], T["ido%d" % t]
+        lm, l0, meta, yo, ido = T.lm, 24 * t, T["meta%d" % t], T["yo%d" % t], T["ido%d" % t]
         land, lans, snd, sns = "land%d" % t, "lans%d" % t, "snd%d" % t, "sns%d" % t
-        mm(1, XQ, 192 * t + 64, CA, (0,), ["xq%d" % t, ca, cas])
-        mm(0, XQ, 192 * t, CA, (0,), ["xq%d" % t, ca, cas])
-        scan(T.mb[64:128, :], ps(1, 0, 128, 64), T.negc[64:128, :], LOW, A.max, A.max, ["ps1", "negc"], ["mb"])
-        scan(T.ma[:, :], ps(0, 0, 128), T.negc[:, :], LOW, A.max, A.max, ["ps0", "negc"], ["ma"])
+        mm(1, XQ, 192 * t + 64, CA, 0, ["xq%d" % t, ca, cas])
+        mm(0, XQ, 192 * t, CA, 0, ["xq%d" % t, ca, cas])
+        scan(T.mb[64:128, :], ps(1, 0, 128, 64), T.cbt[64:128, 128:256], LOW, A.max, A.add, ["ps1", "cbtz"], ["mb"])
+        scan(T.ma[:, :], ps(0, 0, 128), T.cbt[:, 128:256], LOW, A.max, A.add, ["ps0", "cbtz"], ["ma"])
 
-        def before(q, out, m, key, p0, k0, k1, step, wr):
+        def before(q, out, m, key, p0, k0, k1, wr):
             if q == "v":
-                ts(out, m[p0:128, k0:k1:step], m[p0:128, 127:128], None, A.is_lt, None, [key], [wr])
+                ts(out, m[p0:128, k0:k1], m[p0:128, 127:128], None, A.is_lt, None, [key], [wr])
             else:
-                act(out, m[p0:128, k0:k1:step], AF.Sign, m[p0:128, 127:128], -1.0, [key], [wr])
-        if t == 0:
-            await_("s", writers["pt"] + writers["ptx"])
-            await_("v", writers["pt"] + writers["ptx"])
-        before("s", T.pt[:, 4:512:4], T.ma, "ma", 0, 0, 127, 1, "pt0")
-        before("s", T.pt[:, 2:512:4], T.ma, "ma", 0, 0, 128, 1, "pt2")
-        before("v", T.pt[64:128, 5:512:4], T.mb, "mb", 64, 0, 127, 1, "pt1")
-        before("v", T.pt[64:128, 3:512:4], T.mb, "mb", 64, 0, 128, 1, "pt3")
-        before("v", T.ptx[64:128, 5:14:4], T.mb, "mb", 64, 31, 96, 32, "px1")
-        before("v", T.ptx[64:128, 3:12:4], T.mb, "mb", 64, 31, 96, 32, "px3")
-        before("v", T.ptx[:, 4:13:4], T.ma, "ma", 0, 31, 96, 32, "px0")
-        quant("pq", "pqs", 0, 128, "pt", 0, ["pt", "pt0", "pt1", "pt2", "pt3"], ["pq"])
-        before("s", T.ptx[:, 2:11:4], T.ma, "ma", 0, 31, 96, 32, "px2")
-        mm(3, CQ, 128, ("pq", "pqs"), (0,), ["cq", "pq"])
-        mm(2, CQ, 0, ("pq", "pqs"), (0,), ["cq", "pq"])
-        quant("pxq", "pxs", 0, 128, "ptx", 0, ["ptx", "px0", "px1", "px2", "px3"], ["pxq"])
-        mm(6, CQ, 0, ("pxq", "pxs"), (0,), ["cq", "pxq"])
-        mm(7, CQ, 128, ("pxq", "pxs"), (0,), ["cq", "pxq"])
-        for el, c in ((1, 1.0), (3, 2.0)):
-            act(T.zz[64:128, el:512:4], ps(3, 0, 128, 64), AF.Relu, c, -1.0, ["ps3"], ["zz%d" % el])
-        for el, c in ((0, 1.0), (2, 2.0)):
-            ts(T.zz[:, el:512:4], ps(2, 0, 128), c, None, A.is_lt, None, ["ps2"], ["zz%d" % el])
+                act(out, m[p0:128, k0:k1], AF.Sign, m[p0:128, 127:128], -1.0, [key], [wr])
 
-        def below(el, bank, p0):
-            ts(T.zzx[p0:128, el:64:16], ps(bank, 0, 4, p0), CAPP + 1.0, UNIT, A.is_lt, A.mult, ["ps%d" % bank, "zzx"], ["zx%d" % el])
-        below(0, 6, 0)
-        quant("zq", "zqs", 0, 128, "zz", 0, ["zza", "zzb", "zz0", "zz1", "zz2", "zz3"], ["zq"])
-        mm(4, CQ, 256, ("zq", "zqs"), (0,), ["cq", "zq"])
-        mm(5, CQ, 384, ("zq", "zqs"), (0,), ["cq", "zq"])
-        below(1, 7, 64)
-        quant("zxq", "zxs", 0, 128, "zzx", 0, ["zzx", "zx0", "zx1"], ["zxq"])
-        mm(0, CQ, 256, ("zxq", "zxs"), (0,), ["cq", "zxq"])
-        for j, ls in ((0, T.ls1), (1, T.ls2)):
-            scan(ls[:, :], T.msk[:, :], ps(4 + j, 0, 128), 0.0, A.add, A.max, ["ps%d" % (4 + j), "msk"], ["ls%d" % j])
-        for j, ls in ((0, T.ls1), (1, T.ls2)):
-            for h in range(2):
-                act(T.ii[:, 2 * j + h:16:4], ls[:, 15 + 16 * h:128:32], AF.Identity, T.ncorr[:, 0:1], UNIT, ["ls%d" % j, "ncorr"],
-                    ["ii%d%d" % (j, h)])
-            ts(T.lst[:, j:16:2], ls[:, 15:128:16], T.corr[:, 0:1], float(TOK - 1), A.subtract, A.min,
+        def ranks(out, m, key, p0, wr):
+            ts(out, m[p0:128, 31:96:32], m[p0:128, 127:128], 1.0 / 128, A.is_lt, A.mult, [key], [wr])
+        before("s", T.pt[64:128, 5:512:4], T.mb, "mb", 64, 0, 127, "pt1")
+        before("s", T.pt[64:128, 3:512:4], T.mb, "mb", 64, 0, 128, "pt3")
+        ranks(T.pt[64:128, 521:538:8], T.mb, "mb", 64, "px1")
+        ranks(T.pt[64:128, 515:532:8], T.mb, "mb", 64, "px3")
+        before("v", T.pt[:, 4:512:4], T.ma, "ma", 0, 0, 127, "pt0")
+        before("s", T.pt[:, 2:256:4], T.ma, "ma", 0, 0, 64, "pt2")
+        before("v", T.pt[:, 258:512:4], T.ma, "ma", 0, 64, 128, "pt4")
+        ranks(T.pt[:, 520:537:8], T.ma, "ma", 0, "px0")
+        ranks(T.pt[:, 514:531:8], T.ma, "ma", 0, "px2")
+        quant("pq", "pqs", 0, W, "pt", 0, ["pt", "ptr", "pt0c", "pt1c", "pt2c", "pt3c", "pt4c", "pt0", "pt1", "pt2", "pt3", "pt4",
+                                           "px0", "px1", "px2", "px3"], ["pq"])
+        if t == 0:
+            gap_constants(0)
+        else:
+            zero_block(t, 0)
+        if pre:
+            whole_constants(0)
+        mm(2, CQ, 0, ("pq", "pqs"), 0, ["cq", "pq"], W)
+        mm(3, CQ, 128, ("pq", "pqs"), 0, ["cq", "pq"], W)
+        act(T.zz[:, 1:4 * W:4], ps(3, 0, W), AF.Sign, T.thr[:, 0:1], -1.0, ["ps3", "thr"], ["zz1"])
+        for el, c in ((0, ONE), (2, TWO)):
+            ts(T.zz[:, el:4 * W:4], ps(2, 0, W), c, None, A.is_lt, None, ["ps2"], ["zz%d" % el])
+        quant("zq", "zqs", 0, W, "zz", 0, ["zza", "zzb", "zz0", "zz1", "zz2"], ["zq"])
+        if t == 0:
+            gap_constants(1)
+        if pre:
+            whole_constants(1)
+            zero_block(t, 1)
+        mm(4, CQ, 256, ("zq", "zqs"), 0, ["cq", "zq"], W)
+        mm(5, CQ, 384, ("zq", "zqs"), 0, ["cq", "zq"])
+        scan(T.ls[:, 0:W], T.msk[:, 0:W], ps(4, 0, W), 0.0, A.add, A.max, ["ps4", "msk", "mska", "mskb"], ["ls0"])
+        scan(T.ls[:, W:W + 128], T.msk[:, 0:128], ps(5, 0, 128), 0.0, A.add, A.max, ["ps5", "msk"], ["ls1"])
+        two = [T.ls[:, W * j + 32 * far + 15:W * j + 32 * far + 32:16] for j in range(2)]
+
+        def listed(j):
+            ts(T.lst[:, j:16:2], T.ls[:, W * j + 15:W * j + 128:16], T.corr[:, 0:1], float(TOK - 1), A.subtract, A.min,
                ["ls%d" % j, "corr"], ["lst%d" % j])
-        II = ["ii00", "ii01", "ii10", "ii11"]
+        for j in range(2):
+            got = T.ls[:, W * j + 15:W * j + 128:16]
+            act(T.ii[:, j:16:2], got, AF.Identity, T.ncorr[:, 0:1], UNIT, ["ls%d" % j, "ncorr"], ["ii%d" % j])
+            tt(T.flag[:, j:16:2], got, T.ls[:, 128:W], A.is_ge, ["ls0", "ls%d" % j], ["flag%d" % j])
+            if pre:
+                ts(T.pf[:, 2 * j:2 * j + 2], two[j], T.ls[:, 128 + 2 * far:129 + 2 * far], (512.0, T.b1[:, 0:1])[j], A.is_ge, A.mult,
+                   ["ls0", "ls%d" % j, "b1"], ["pf%d" % j])
+            else:
+                listed(j)
+        if pre:
+            for h in range(2):
+                x = 32 * far + 16 * h + 15
+                ts(T.pg[:, h:h + 1], T.ls[:, x:x + 1], T.b0[:, 0:1], T.pf[:, h:h + 1], A.add, A.add, ["ls0", "b0", "pf0"], ["pg%d" % h])
+            tt(T.pg[:, 2:4], two[1], T.pf[:, 2:4], A.max, ["ls1", "pf1"], ["pg2"])
         LST = ["lst0", "lst1"]
         mk = "meta%d" % t
-        sp0, sp1 = split(rank, 0), split(rank, 1)
-        me = slice(64 * rank, 64 * rank + 64)
         ark = "ark%d" % t
 
         def slots(kind, n):
@@ -369,145 +422,169 @@ def rank_program(g, core, T, topo):
             if n < 3:
                 pick(kind, b, 64 * n, 64, x, 192 * t, 192 * t + 192, "lst", 4 * d, LST + ["xq%d" % t], ["%s.%d" % (b, n)])
             else:
-                pick(kind, o, 64 * rank, 64, x, 192 * t, 192 * t + 192, "lst", 4 * d, LST + ["xq%d" % t], [o])
-
-        def send_codes(n):
-            remote([one(oth[n], T[snd][:, 64 * n:64 * n + 64].bitcast(dt.uint8), T[land][:, me].bitcast(dt.uint8), ark, full)],
-                   ["%s.%d" % (snd, n)])
+                pick(kind, o, column(rank, rank, t), 64, x, 192 * t, 192 * t + 192, "lst", 4 * d, LST + ["xq%d" % t], [o + "o"])
 
         def place(d):
-            e = [s for s in range(N) if s != d].index(rank)
-            return slice(8 + 4 * e, 12 + 4 * e)
-        for n in range(4):
+            e = senders(d, t).index(rank)
+            return slice(l0 + 8 + 4 * e, l0 + 12 + 4 * e)
+        tt(meta[:, :], T.ii[:, :], T.flag[:, :], A.add, ["ii0", "ii1", "flag0", "flag1"], [mk])
+        if pre:
+            listed(0)
+            for h in range(2):
+                ts(T.pv[:, h:h + 1], T.pg[:, 2 + h:3 + h], 256.0, T.pg[:, h:h + 1], A.mult, A.add, ["pg%d" % h, "pg2"], ["pv%d" % h])
+            listed(1)
+        for d in (oth[1:] + [far] if pre else oth):
+            if pre and d == far:
+                remote([d], T.pv[:, :], T.pk[:, :], "arf", ["pv0", "pv1"])
+            else:
+                remote([d], meta[:, 4 * d:4 * d + 4], lm[:, place(d)], "arm%d" % t, [mk])
+        for n in range(int(pre), 4):
             slots("s", n)
-        scan(T.cut[:, :], T.hold[:, :], ps(0, 0, 16), 0.0, A.min, A.add, ["hold", "ps0"], ["cut"])
-        slots("c", 0)
-        send_codes(0)
-        tt(T.flag[:, :], T.ii[:, :], T.cut[:, :], A.is_ge, II + ["cut"], ["flag"])
-        slots("c", 1)
-        tt(meta[:, :], T.ii[:, :], T.flag[:, :], A.add, II + ["flag"], [mk])
-        remote([one(d, meta[:, 4 * d:4 * d + 4], lm[:, place(d)], "arm%d" % t, sp0[d]) for d in oth], [mk])
-        send_codes(1)
-        slots("c", 2)
-        remote([one(e, T[sns][:, 64 * m:64 * m + 64], T[lans][:, me], ark, sp1[e]) for m, e in enumerate(oth)],
-               ["%s.%d" % (sns, m) for m in range(3)])
-        send_codes(2)
+        for n, d in enumerate(oth):
+            if pre and d == far:
+                continue
+            me = slice(column(d, rank, t), column(d, rank, t) + 64)
+            slots("c", n)
+            remote([d], T[snd][:, 64 * n:64 * n + 64].bitcast(dt.uint8), T[land][:, me].bitcast(dt.uint8), ark, ["%s.%d" % (snd, n)])
+            remote([d], T[sns][:, 64 * n:64 * n + 64], T[lans][:, me], ark, ["%s.%d" % (sns, n)],
+                   "left" if (t, n) == (0, 2) else "sent")
+        if t == 0:
+            await_("y", [("left", len(full), {"left": len(full)}, "r")])
+            dma("y", T.xt[:, 1536:2304], T.x[:, 1536:2304], [], ["xt2"], "ldx2")
         slots("c", 3)
-        if t == 0:
-            for b in range(4):
-                quant("eq", "eqs", 128 * b, 128 * b + 128, "et", 520 * (b % 2) + 2 - 2 * (b // 2), ["etz", "et%d" % (b % 2)],
-                      ["eq%d" % b])
+        run("v", lambda e: e.tensor_copy(lm[:, l0:l0 + 4], meta[:, 4 * rank:4 * rank + 4]), [mk, "lp"], ["lo%d" % t])
         for b in range(4):
-            mm(4 + b, EQ, 128 * b, CA, (0,), ["eq%d" % b, ca, cas])
-        if t == 0:
-            act(T.hc[:, 128:256], T.cbt[:, 0:128], AF.Copy, 0.0, 1.0, ["cbt"], ["ho"])
-        else:
-            act(T.hc[:, 128:256], T.nt[:, 0:128], AF.Copy, 0.0, 1.0, NT, ["ho"])
+            mm(4 + b, EQ, 128 * b, CA, 0, ["eq%d" % b, ca, cas])
+        act(T.hc[:, 0:384:3], (T.cbt if t == 0 else T.nt)[:, 0:128], AF.Copy, 0.0, 1.0, ["cbt"] if t == 0 else NT, ["ho"])
         for b in range(4):
-            act(T.hc[:, b:128:4], ps(4 + b, G * rank, G * rank + G), AF.Copy, 0.0, 2.0, ["ps%d" % (4 + b)], ["hc%d" % b])
-        run("v", lambda e: e.tensor_copy(lm[:, 0:4], meta[:, 4 * rank:4 * rank + 4]), [mk], ["lo%d" % t])
-        if t == 0:
-            late_constants()
-        arrive("arm%d" % t, n_meta, ["lm%d" % t])
-        LM = ["lm%d" % t, "lo%d" % t, "lp%d" % t]
-        DD = ["dq0", "dq1"] + ["dd%d" % i for i in range(9)]
+            act(T.hc[:, 3 * b + 2:384:12], ps(4 + b, G * rank, G * rank + G), AF.Copy, 0.0, 2.0, ["ps%d" % (4 + b)], ["hc%d" % b])
+        LM = ["lm%d" % t, "lo%d" % t, "lp"]
+        DD, dd = STEPS, T.dd
+        if pre:
+            arrive("arf", len(common(far)), ["pk"])
+            ts(T.ur[:, :], T.pk[:, :], 1.0 / 256, None, A.mult, None, ["pk"], ["ur"])
+            ts(T.uf[:, :], T.pk[:, :], 256.0 * TOK + 128, None, A.is_ge, None, ["pk"], ["uf"])
+            ts(T.ug[:, :], T.pk[:, :], 1.0 / 512, None, A.mult, None, ["pk"], ["ug"])
+            ts(T.um[:, :], T.ur[:, :], TOK + 1.0, -0.5, A.min, A.mult, ["ur"], ["um"])
+            for h in range(2):
+                ts(lm[:, l0 + 17 + 2 * h:l0 + 18 + 2 * h], T.ur[:, h:h + 1], 1.0 / 512, T.uf[:, h:h + 1], A.mult, A.add,
+                   ["ur", "uf", "lp"], ["lf%d" % h])
+            tt(lm[:, l0 + 16:l0 + 20:2], T.ug[:, :], T.um[:, :], A.add, ["ug", "um", "lp"], ["lf2"])
+            LM += ["lf0", "lf1", "lf2"]
+            DD, dd = ["de%d" % i for i in range(8)], T.de
+        arrive("arm%d" % t, n_meta - (len(common(far)) if pre else 0), ["lm%d" % t])
+        seen = [lm[:, l0 + 2 * h:l0 + 2 * h + 18] for h in range(2)]
         for h in range(2):
-            scan(T.ab[:, 2 + h:22:2], lm[:, h:20:2], T.dd[:, 10 * h:10 * h + 10], FAR, A.min, A.add, LM + DD, ["ab%d" % (1 + h)])
+            scan(T.ab[:, 4 + 2 * h:76:4], seen[h], dd[:, 20 * h:20 * h + 18], FAR, A.min, A.add, LM + DD, ["fa%d" % h])
         for h in range(2):
-            act(T.junk[:, 10 * h:10 * h + 10], lm[:, h:20:2], AF.Sign, 0.75, -1.0, LM, ["cs%d" % h], T.cs[:, h:h + 1])
-        tt(T.mx[:, 0:20], lm[:, :], T.ab[:, 0:20], A.max, LM + ["ab0", "ab1", "ab2"], ["mx"])
-        F, S = T.ab[:, 20:22], T.sec[:, 9:20:10]
-        ts(T.f5[:, :], F, 512.0, None, A.mult, None, ["ab1", "ab2"], ["f5"])
-        ts(T.alst[:, 2:4], F, 512.0, None, A.mult, None, ["ab1", "ab2"], ["alst1"])
+            scan(T.cn[:, 20 * h:20 * h + 18], seen[h], T.cc[:, 0:18], 0.0, A.add, A.mult,
+                 LM + ["cc0", "cc1", "cc2", "cc3"], ["cn%d" % h])
         for h in range(2):
-            scan(T.sec[:, 10 * h:10 * h + 10], T.mx[:, h:20:2], T.dd[:, 10 * h:10 * h + 10], FAR, A.min, A.add, ["mx"] + DD, ["sc%d" % h])
-        ts(T.v2[:, :], T.cs[:, :], -7.0, 512.0, A.is_ge, A.mult, ["cs0", "cs1"], ["v2"])
-        ts(T.mv[:, :], F, 1.0, 128.0, A.is_ge, A.mult, ["ab1", "ab2"], ["mv"])
+            tt(T.mx[:, 20 * h:20 * h + 18], seen[h], T.ab[:, 2 * h:72:4], A.max, LM + ["ab", "fa%d" % h], ["mx%d" % h])
+        F, S = T.ab[:, 72:76:2], T.ab[:, 73:76:2]
+        FK, SK = ["fa0", "fa1"], ["sc0", "sc1"]
+        act(T.f5[:, :], F, AF.Copy, 0.0, 512.0, FK, ["f5"])
+        act(T.mv[:, :], F, AF.Sign, 0.875, -1.0, FK, ["mv"])
+        ts(T.alst[:, 2:4], F, 512.0, None, A.mult, None, FK, ["alst1"])
+        ts(T.v2[:, :], T.cn[:, 17:40:20], 2 * PAD + 6.7, 512.0, A.is_lt, A.mult, ["cn0", "cn1"], ["v2"])
         for h in range(2):
-            ts(T.alst[:, h:h + 1], T.sec[:, 10 * h + 9:10 * h + 10], T.v2[:, h:h + 1], T.f5[:, h:h + 1], A.mult, A.max,
+            scan(T.ab[:, 5 + 2 * h:76:4], T.mx[:, 20 * h:20 * h + 18], dd[:, 20 * h:20 * h + 18], FAR, A.min, A.add,
+                 ["mx%d" % h] + DD, ["sc%d" % h])
+
+        def base(h):
+            ts(T.blst[:, h:8:2], T.k8[:, h:8:2], T.mv[:, h:h + 1], T.q4[:, 0:1], A.add, A.add, ["k8", "mv", "q4"], ["blst%d" % h])
+        base(0)
+        for h in range(2):
+            ts(T.alst[:, h:h + 1], T.ab[:, 73 + 2 * h:74 + 2 * h], T.v2[:, h:h + 1], T.f5[:, h:h + 1], A.mult, A.max,
                ["sc%d" % h, "v2", "f5"], ["alst0%d" % h])
 
-        def numbers1():
-            for i, (k, keys) in enumerate(((F, ["ab1", "ab2"]), (S, ["sc0", "sc1"]))):
-                ts(T.vi[:, 2 * i:2 * i + 2], k, 1.0 / UNIT, None, A.mult, None, keys, ["vi%d" % i])
-                act(T.sg[:, 2 * i:2 * i + 2], k, AF.Sign, 0.75, -1.0, keys, ["sg%d" % i])
-            act(T.wv[:, :], T.sg[:, :], AF.Identity, 2047.5, 2048.5, ["sg0", "sg1"], ["wv"])
-            ts(T.sv[:, :], T.vi[:, :], 15, None, A.arith_shift_right, None, ["vi0", "vi1"], ["sv"])
-            ts(T.iv[:, :], T.vi[:, :], 511, None, A.bitwise_and, None, ["vi0", "vi1"], ["iv"])
+        def second():
+            ts(T.alst[:, 4:6], S, 512.0, None, A.mult, None, SK, ["alst2"])
 
-        def numbers2():
-            ts(T.s192[:, :], T.sv[:, :], float(TOK), None, A.mult, None, ["sv"], ["s192"])
-            tt(T.idf[:, :], T.s192[:, :], T.iv[:, :], A.add, ["s192", "iv"], ["idf"])
+        def numbers(step):
+            keys = T.ab[:, 72:76]
+            if step == 0:
+                act(T.sg[:, :], keys, AF.Sign, 0.875, -1.0, FK + SK, ["sg"])
+            elif step == 1:
+                ts(T.vi[:, :], keys, 1.0 / UNIT, 2048.0 * column(rank, far, t) * pre, A.mult, A.subtract, FK + SK, ["vi"])
+            elif step == 2:
+                act(T.wv[:, :], T.sg[:, :], AF.Identity, 2047.5, 2048.5, ["sg"], ["wv"])
+            elif step == 3:
+                if pre:
+                    ts(T.col[:, :], T.vi[:, :], 11, None, A.arith_shift_right, None, ["vi"], ["col"])
+                ts(T.iv[:, :], T.vi[:, :], 2047, None, A.bitwise_and, None, ["vi"], ["iv"])
+                if pre:
+                    ts(T.z1[:, :], T.col[:, :], 0.0, float(TOK), A.max, A.min, ["col"], ["z1"])
+                    tt(T.z4[:, :], T.z1[:, :], T.iv[:, :], A.add, ["z1", "iv"], ["z4"])
+            else:
+                tt(ido[:, :], T.wv[:, :], (T.z4 if pre else T.iv)[:, :], A.min, ["iv", "z4", "wv"], ["ido%d" % t])
+                for h in range(2):
+                    dma("y", T.ids[0:1, 64 * t + 32 * h:64 * t + 32 * h + 32], ido[0:16, 2 * h:2 * h + 2], ["ido%d" % t], [], "st")
 
-        def numbers3():
-            for i in range(2):
-                tt(ido[:, i:4:2], T.idf[:, 2 * i:2 * i + 2], T.wv[:, 2 * i:2 * i + 2], A.min, ["idf", "wv"], ["ido%d%d" % (t, i)])
-            for h in range(2):
-                dma("s" if last and h else "y", T.ids[0:1, 64 * t + 32 * h:64 * t + 32 * h + 32], ido[0:16, 2 * h:2 * h + 2],
-                    ["ido%d0" % t, "ido%d1" % t], [], "st")
-
-        def outputs():
-            if t == 0:
-                quant("wq", "ws", 0, 128, "wt", 0, ["wt"], ["wq"])
-                quant("ady", "adys", 0, 128, "cbt", 128, ["cbtz"], ["ady", "adys"])
-            pick("c", "ady", 0, 64, land, 0, 640, "alst", 2, AL + ["alst2", land], ["ady"])
-            pick("s", "adys", 0, 64, lans, 0, 640, "alst", 2, AL + ["alst2", lans], ["adys"])
-            mm(6, ("wq", "ws"), 0, ("ady", "adys"), (0,), ["wq", "ady", "adys"])
+        def store_y():
+            mm(6, ("wq", "ws"), 0, ("ady", "adys"), 0, ["wq", "ady", "adys"])
             for i in range(2):
                 act(yo[:, i:64:2], ps(6, 32 * i, 32 * i + 32), AF.Copy, 0.0, 1.0, ["ps6"], ["yo%d%d" % (t, i)])
             dma("y", T.y[:, 64 * t:64 * t + 64], yo[:, :], ["yo%d0" % t, "yo%d1" % t], [], "st")
-        ts(T.alst[:, 4:6], S, 512.0, None, A.mult, None, ["sc0", "sc1"], ["alst2"])
-        if last:
-            numbers1()
         arrive(ark, n_tok, [land, lans])
-        AL = ["alst00", "alst01", "alst1", "lz%d" % t]
-        pick("c", "adm", 0, 64, land, 0, 640, "alst", 0, AL + [land], ["adm"])
-        pick("s", "adms", 0, 64, lans, 0, 640, "alst", 0, AL + [lans], ["adms"])
-        for h in range(2):
-            ts(T.blst[:, h:8:2], T.k8[:, h:8:2], T.mv[:, h:h + 1], T.q4[:, 0:1], A.add, A.add, ["k8", "mv", "q4"], ["blst%d" % h])
-        run("v", lambda e: e.tensor_copy(T.hb[:, :], T.hc[:, 0:256].indirect(T.blst[:, 0:8])),
-            ["blst0", "blst1", "ho", "hc0", "hc1", "hc2", "hc3"], ["hb"])
-        for b, ras in ((2, (0,)), (3, (0,)), (0, (0, 32)), (1, (0, 32))):
-            mm(b, EQ, 128 * b, ("adm", "adms"), ras, ["eq%d" % b, "adm", "adms"])
-        for b in (2, 3):
-            act(T.s4[:, 32 * b:32 * b + 32], ps(b, 32, 64), AF.Copy, 0.0, 1.0, ["ps%d" % b], ["s4%d" % b])
-        if last:
-            outputs()
-            numbers2()
-        if t == 0:
-            await_("v", writers["nt"])
+        AL = ["alst1", "lz%d0" % t] + (["lz%d1" % t] if pre else [])
+        end = 768 if pre else 640
+        for i, keys in ((1, []), (0, ["alst00", "alst01"])):
+            pick("c", "adm", 32 * i, 32, land, 0, end, "alst", 2 * i, AL + keys + [land, land + "o", "adm"], ["adm%d" % i])
+            pick("s", "adms", 32 * i, 32, lans, 0, end, "alst", 2 * i, AL + keys + [lans, lans + "o", "adms"], ["adms%d" % i])
+        base(1)
 
-        def half(b, part, key):
-            tt(T.nt[:, b:128:4], part, T.hb[:, 32 * b:32 * b + 32], A.add, [key, "hb"], ["nt%d" % b])
-        for b in (2, 3):
-            tt(T.hh[:, 32 * b:32 * b + 32], ps(b, 0, 32), T.s4[:, 32 * b:32 * b + 32], A.add, ["ps%d" % b, "s4%d" % b], ["hh%d" % b])
-        half(0, ps(0, 0, 32), "ps0")
-        half(2, T.hh[:, 64:96], "hh2")
-        half(3, T.hh[:, 96:128], "hh3")
-        half(1, ps(1, 0, 32), "ps1")
+        def for_y():
+            pick("c", "ady", 0, 64, land, 0, end, "alst", 2, AL + ["alst2", land, land + "o"], ["ady"])
+            pick("s", "adys", 0, 64, lans, 0, end, "alst", 2, AL + ["alst2", lans, lans + "o"], ["adys"])
+        if last:
+            second()
+            numbers(0)
+        run("v", lambda e: e.tensor_copy(T.hb[:, :], T.hc[:, 0:384].indirect(T.blst[:, 0:8])),
+            ["blst0", "blst1", "ho", "hc0", "hc1", "hc2", "hc3"], ["hb"])
+        for i in (1, 0):
+            for b in range(4):
+                mm(b, EQ, 128 * b, ("adm", "adms"), 32 * i, ["eq%d" % b, "adm1", "adms1", "adm%d" % i, "adms%d" % i], part=i)
+        if last:
+            for_y()
+            numbers(2)
+            numbers(1)
+        for b in range(4):
+            tt(T.nt[:, b:128:4], ps(b, 0, 32), T.hb[:, 32 * b:32 * b + 32], A.add, ["ps%d" % b, "hb"], ["nt%d" % b])
+            if last and b == 0:
+                numbers(3)
+        if last:
+            numbers(4)
+            store_y()
         nk = ca + "n"
         run("v", lambda e: e.quantize_mx(T[ca][:, 128:256], T[cas][:, 128:256], T.nt[:, :]), ["nt"] + NT, [nk])
         if last:
             dma("y", T.oc[:, :], T[ca][:, new].bitcast(dt.uint8), [nk], [], "st")
             for k in range(4):
                 dma("y" if k == 3 else "s", T.osc[4 * k:4 * k + 4, :], T[cas][32 * k:32 * k + 4, new], [nk], [], "st")
-            numbers3()
         else:
             cn, cns = "ca%d" % (t + 1), "cas%d" % (t + 1)
-            remote([many(T[ca][:, new].bitcast(dt.uint8), T[cn][:, own].bitcast(dt.uint8), "arc%d" % (t + 1))], [nk])
-            remote([many(T[cas][:, new], T[cns][:, own], "arc%d" % (t + 1))], [nk])
+            send_centroids(ca, cas, new, t + 1, nk)
+            second()
             quant("xq", "xs", 192 * t + 192, 192 * t + 384, "xt", 768 * t + 768, ["xt%d" % (t + 1)], ["xq%d" % (t + 1)])
+            if t + 1 == PRE:
+                a, x = column(far, rank, PRE), TOK * PRE
+                remote([far], T.xq[:, x:x + TOK].bitcast(dt.uint8), T["land%d" % PRE][:, a:a + TOK].bitcast(dt.uint8), "ark%d" % PRE,
+                       ["xq%d" % PRE])
+                remote([far], T.xs[:, x:x + TOK], T["lans%d" % PRE][:, a:a + TOK], "ark%d" % PRE, ["xq%d" % PRE])
             pick("c", cn, G * rank, G, ca, 128, 256, "ilst", 0, [nk, "ilst0", "ilst1"], [cn])
             pick("s", cns, G * rank, G, cas, 128, 256, "ilst", 0, [nk, "ilst0", "ilst1"], [cns])
-            outputs()
-            numbers1()
-            zero_block(t + 1)
-            numbers2()
-            numbers3()
-            arrive("arc%d" % (t + 1), n_cen, [cn, cns])
             if t == 0:
-                await_("y", writers["ca1"])
-                dma("y", T.xt[:, 1536:2304], T.x[:, 1536:2304], [], ["xt2"], "ldx2")
+                quant("wq", "ws", 0, 128, "wt", 0, ["wt"], ["wq"])
+            arrive("arc%d" % (t + 1), n_cen, [cn, cns])
+            await_("y", writers[cn])
+            numbers(0)
+            numbers(1)
+            for_y()
+            numbers(2)
+            numbers(3)
+            store_y()
+            numbers(4)
     for k in cnt:
         if know["p"].get(k, 0) < cnt[k]:
             g.wait_ge(T.sem[k], cnt[k])

from concourse.bass import DstId, RemoteDMATransfer
from concourse.mybir import dt, AluOpType as A, ActivationFunctionType as AF

CODE = "float8_e4m3fn_x4"
N, G, TOK, R, CAPP = 4, 32, 192, 3, 64
UNIT = 2.0 ** -20
WIN = 512
FAR = 64.0
LOW = -1.0e29
LIFT = 256.0
W = 136
PAD = 8.0
BIG = 1024.0
ONE, TWO = (CAPP + 0.5) / 128, 1.5
PRE = 1

SCRATCH = {
    "cbt": ("sbuf", [128, 768], "bfloat16"), "xt": ("sbuf", [128, 2304], "bfloat16"), "wt": ("sbuf", [128, 512], "bfloat16"),
    "pt": ("sbuf", [128, 4 * W], "bfloat16"), "zz": ("sbuf", [128, 4 * W], "bfloat16"),
    "nt": ("sbuf", [128, 512], "bfloat16"), "ct": ("sbuf", [128, 2048], "bfloat16"), "et": ("sbuf", [128, 1040], "bfloat16"),
    "ps": ("psum", [128, 4096], "float32"), "hc": ("sbuf", [128, 384], "float32"), "ls": ("sbuf", [128, 2 * W], "float32"),
    "msk": ("sbuf", [128, W], "float32"), "ab": ("sbuf", [128, 80], "float32"), "lm": ("sbuf", [128, 24 * R], "bfloat16"),
}
for _c, _s, _n in (("cq", "cqs", 512), ("eq", "eqs", 512), ("cbq", "cbs", 128), ("xq", "xs", 576), ("wq", "ws", 128),
                   ("pq", "pqs", W), ("zq", "zqs", W), ("adm", "adms", 160), ("ady", "adys", 128)):
    SCRATCH[_c] = ("sbuf", [128, _n], CODE)
    SCRATCH[_s] = ("sbuf", [128, _n], "uint8")
for _b in ("rowi", "k16", "mk1", "ma", "mb", "dist", "hb"):
    SCRATCH[_b] = ("sbuf", [128, 128], "float32")
for _b in ("pcol", "lo5", "hi5", "thr", "npcol", "qcol", "q1", "b0", "b1", "corr", "ncorr", "q4"):
    SCRATCH[_b] = ("sbuf", [128, 1], "float32")
for _b in ("dd", "de", "mx", "cn", "cc"):
    SCRATCH[_b] = ("sbuf", [128, 40], "float32")
for _b in ("v2", "f5", "mv", "ug", "uf", "um"):
    SCRATCH[_b] = ("sbuf", [128, 2], "float32")
for _b in ("sg", "wv", "pf", "pg", "z1", "z4"):
    SCRATCH[_b] = ("sbuf", [128, 4], "float32")
for _b, _n, _d in (("pi", 1, "int32"), ("qi", 1, "int32"), ("ii", 16, "float32"), ("flag", 16, "float32"), ("lst", 16, "uint16"),
                   ("alst", 6, "uint16"), ("blst", 8, "uint16"), ("ilst", 2, "uint16"), ("k8", 8, "float32"),
                   ("vi", 4, "int32"), ("iv", 4, "int32"), ("col", 4, "int32"), ("ur", 2, "int32"), ("pv", 2, "uint16"),
                   ("pk", 2, "uint16")):
    SCRATCH[_b] = ("sbuf", [128, _n], _d)
for _t in range(R):
    SCRATCH["meta%d" % _t] = ("sbuf", [128, 16], "bfloat16")
    SCRATCH["snd%d" % _t] = ("sbuf", [128, 192], CODE)
    SCRATCH["sns%d" % _t] = ("sbuf", [128, 192], "uint8")
    SCRATCH["land%d" % _t] = ("sbuf", [128, 768], CODE)
    SCRATCH["lans%d" % _t] = ("sbuf", [128, 768], "uint8")
    SCRATCH["yo%d" % _t] = ("sbuf", [128, 64], "float32")
    SCRATCH["ido%d" % _t] = ("sbuf", [128, 4], "float32")
    SCRATCH["ca%d" % _t] = ("sbuf", [128, 256], CODE)
    SCRATCH["cas%d" % _t] = ("sbuf", [128, 256], "uint8")
SEMAPHORES = ["qv", "qs", "qt", "qp", "ldcb", "ldx0", "ldx1", "ldx2", "ldw", "st", "sent", "left", "arf",
              "arc0", "arc1", "arc2", "arm0", "arm1", "arm2", "ark0", "ark1", "ark2"]


def rank_program(g, core, T, topo):
    rank = T.rank_of(core)
    if rank is None:
        return
    cores = list(T.cores)

    def others(r):
        def hops(d):
            a, b = topo.chip(cores[r]), topo.chip(cores[d])
            return 1 if topo.mates(a, b) or topo.same_plane(a, b) else 2
        return sorted([d for d in range(N) if d != r], key=lambda d: -hops(d))

    def bits(es):
        m = 0
        for e in es:
            m |= 1 << e
        return m

    def common(r):
        es = topo.engines(cores[r], cores[others(r)[0]])
        for d in others(r):
            es = [e for e in es if e in topo.engines(cores[r], cores[d])]
        return es

    oth = others(rank)
    far = oth[0]
    full = common(rank)
    dst = {}
    for d in oth:
        rid, pid, _ = topo.addr(cores[d])
        dst[d] = (rid, pid)
    n_meta = sum(len(common(s)) for s in range(N) if s != rank)
    n_tok = 2 * n_meta
    n_cen = 2 * n_meta

    def senders(d, t):
        return sorted(others(d)[1:]) + others(d)[:1] if t == PRE else sorted(others(d))

    def column(d, s, t):
        return 64 * s + (TOK - 64 if t == PRE and s > others(d)[0] else 0)

    def keys_at(t):
        return [column(rank, s, t) / 512 + (s - (t == PRE and s > far)) * TOK * UNIT for s in [rank] + senders(rank, t)]

    ENG = {"v": g.vector, "s": g.scalar, "t": g.tensor, "p": g, "y": g.sync}
    cnt = {}
    know = {q: {} for q in ENG}
    writers, readers = {}, {}

    def await_(q, recs):
        recs = [r for r in recs if know[q].get(r[0], 0) < r[1]]
        keep = []
        for i, r in enumerate(recs):
            if any(o is not r and o[2].get(r[0], 0) >= r[1] and not (o[0] == r[0] and o[1] == r[1] and j > i)
                   for j, o in enumerate(recs)):
                continue
            keep.append(r)
        for r in keep:
            if know[q].get(r[0], 0) < r[1]:
                ENG[q].wait_ge(T.sem[r[0]], r[1])
            for k, v in r[2].items():
                know[q][k] = max(know[q].get(k, 0), v)
        for r in recs:
            for k, v in r[2].items():
                know[q][k] = max(know[q].get(k, 0), v)

    def deps(q, rd, wr):
        recs = []
        for k in rd:
            recs += [r for r in writers.get(k, [])]
            if k[:2] == "ps":
                recs += [r for r in readers.get(k, []) if r[3] != q]
        for k in wr:
            recs += writers.get(k, []) + readers.get(k, [])
        return recs

    def note(rec, rd, wr):
        for k in wr:
            writers[k], readers[k] = [rec], []
        for k in rd:
            if k not in wr:
                readers.setdefault(k, []).append(rec)

    def record(q, sem, n):
        cnt[sem] = cnt.get(sem, 0) + n
        clk = dict(know[q])
        clk[sem] = cnt[sem]
        return (sem, cnt[sem], clk, q)

    def run(q, f, rd, wr):
        await_(q, deps(q, rd, wr))
        f(ENG[q]).then_inc(T.sem["q" + q], 1)
        note(record(q, "q" + q, 1), rd, wr)

    def dma(q, out, in_, rd, wr, sem):
        await_(q, deps(q, rd, wr))
        ENG[q].dma_start(out, in_).then_inc(T.sem[sem], 16)
        note(record(q, sem, 16), rd, wr)

    def arrive(sem, n, keys):
        cnt[sem] = n
        rec = (sem, n, {sem: n}, "r")
        for k in keys:
            writers.setdefault(k, []).append(rec)

    def remote(ds, src, to, sem, rd, left="sent"):
        await_("p", deps("p", rd, []))
        g.remote_dma_fused([RemoteDMATransfer(dst_ids=[DstId(rid=dst[d][0], pnc=dst[d][1]) for d in ds],
                                              dma_engine_mask=bits(full), remote_sem=T.sem[sem],
                                              srcs=[src], dsts=[to for d in ds])], local_sem=T.sem[left])
        cnt[left] = cnt.get(left, 0) + len(full)

    def ts(out, in0, s1, s2, o0, o1, rd, wr):
        if o1 is None:
            run("v", lambda e: e.tensor_scalar(out, in0, s1, None, o0), rd, wr)
        else:
            run("v", lambda e: e.tensor_scalar(out, in0, s1, s2, o0, o1), rd, wr)

    def tt(out, a, b, op, rd, wr):
        run("v", lambda e: e.tensor_tensor(out, a, b, op), rd, wr)

    def scan(out, a, b, first, o0, o1, rd, wr):
        run("v", lambda e: e.tensor_tensor_scan(out, a, b, first, o0, o1), rd, wr)

    def act(out, in_, func, bias, scale, rd, wr):
        run("s", lambda e: e.activation(out, in_, func, bias=bias, scale=scale), rd, wr)

    def fill(ap, c, key):
        run("v", lambda e: e.memset(ap, c), [], [key])

    def flat(out, in_, c, rd, key):
        act(out, in_, AF.Identity, c, 0.0, rd, [key])

    def quant(c, s, a, b, tile, x, keys, out):
        run("v", lambda e: e.quantize_mx(T[c][:, a:b], T[s][:, a:b], T[tile][:, x:x + 4 * (b - a)]), keys, out)

    def mm(bank, l, la, r, ra, rd, n=128, part=None):
        lc, lsc = l
        rc, rs = r
        await_("t", deps("t", rd, [] if part == 0 else ["ps%d" % bank]))
        g.tensor.matmul_mx(T.ps[:, 512 * bank:512 * bank + n], T[lc][:, la:la + 128], T[lsc][:, la:la + 128],
                           T[rc][:, ra:ra + n], T[rs][:, ra:ra + n], part != 0, part != 1).then_inc(T.sem["qt"], 1)
        note(record("t", "qt", 1), rd, ["ps%d" % bank])

    def pick(kind, dstb, da, n, srcb, sa, sb, lstb, la, rd, wr):
        k = n // 16
        if kind == "c":
            run("v", lambda e: e.tensor_copy(T[dstb][:, da:da + n].bitcast(dt.uint32),
                                             T[srcb][:, sa:sb].bitcast(dt.uint32).indirect(T[lstb][:, la:la + k])), rd, wr)
        else:
            run("s", lambda e: e.activation(T[dstb][:, da:da + n],
                                            T[srcb][:, sa:sb].indirect(T[lstb][:, la:la + k]), AF.Copy), rd, wr)

    def iota(out, pattern, base, mult, key, imprecise=True):
        if imprecise:
            run("p", lambda e: e.iota(out, pattern, base, mult, allow_small_or_imprecise_dtypes=True), [], [key])
        else:
            run("p", lambda e: e.iota(out, pattern, base, mult), [], [key])

    def ps(bank, a, b, p0=0):
        return T.ps[p0:128, 512 * bank + a:512 * bank + b]

    dma("y", T.cbt[:, 0:128], T.cb[:, :], [], ["cbt"], "ldcb")
    dma("y", T.xt[:, 0:768], T.x[:, 0:768], [], ["xt0"], "ldx0")

    iota(T.pi[:, :], [[1, 1]], 0, 1, "pi", False)
    iota(T.rowi[:, :], [[1, 128]], 0, 0, "rowi")
    iota(T.pcol[:, :], [[1, 1]], 0, 1, "pcol")
    fill(T.cbt[:, 128:768], 0.0, "cbtz")
    fill(T.lm[:, :], PAD, "lp")
    ts(T.qi[:, :], T.pi[:, :], 15, None, A.bitwise_and, None, ["pi"], ["qi"])
    fill(T.ct[:, 1:512:2], 0.0, "ct0c")
    fill(T.ct[0:64, 513:1024:2], 0.0, "ct1e")
    run("v", lambda e: e.tensor_copy(T.qcol[:, :], T.qi[:, :]), ["qi"], ["qcol"])
    fill(T.pt[0:64, 1:512:2], 0.0, "pt")
    fill(T.zz[:, 3:4 * W:4], 0.0, "zza")
    flat(T.ct[:, 512:1024:4], T.rowi[:, :], 1.0, ["rowi"], "ct1a")
    flat(T.ct[:, 514:1024:4], T.rowi[:, :], -1.0, ["rowi"], "ct1b")
    for i, c in ((0, 1.0), (2, 0.0), (3, 0.0)):
        flat(T.ct[:, 1024 + i:1536:4], T.rowi[:, :], c, ["rowi"], "ct2%d" % i)

    quant("cbq", "cbs", 0, 128, "cbt", 0, ["cbt", "cbtz", "lp"], ["cbq"])
    own = slice(G * rank, G * rank + G)
    new = slice(128, 128 + G)

    def send_centroids(c, s, cols, t, key):
        remote(oth, T[c][:, cols].bitcast(dt.uint8), T["ca%d" % t][:, own].bitcast(dt.uint8), "arc%d" % t, [key])
        remote(oth, T[s][:, cols], T["cas%d" % t][:, own], "arc%d" % t, [key])
    send_centroids("cbq", "cbs", slice(0, G), 0, "cbq")
    for h in range(2):
        ts(T.ilst[:, h:h + 1], T.qcol[:, :], 16.0 * h, None, A.add, None, ["qcol"], ["ilst%d" % h])
    ts(T.lo5[:, :], T.pcol[:, :], 64.0, 0.5, A.is_lt, A.mult, ["pcol"], ["lo5"])
    ts(T.hi5[:, :], T.pcol[:, :], 64.0, 0.5, A.is_ge, A.mult, ["pcol"], ["hi5"])
    fill(T.pt[:, 512:4 * W], 0.0, "ptr")
    pick("c", "ca0", G * rank, G, "cbq", 0, 128, "ilst", 0, ["cbq", "ilst0", "ilst1"], ["ca0"])
    pick("s", "cas0", G * rank, G, "cbs", 0, 128, "ilst", 0, ["cbq", "ilst0", "ilst1"], ["cas0"])
    arrive("arc0", n_cen, ["ca0", "cas0"])
    iota(T.k16[:, :], [[0, 8], [1, 16]], 0, 0, "k16")
    iota(T.et[:, :], [[0, 1040]], 0, 0, "etz")
    iota(T.k8[:, :], [[3, 4], [192, 2]], 1, 0, "k8")
    ts(T.npcol[:, :], T.pcol[:, :], -1.0, None, A.mult, None, ["pcol"], ["npcol"])
    flat(T.ct[:, 1025:1536:4], T.rowi[:, :], T.lo5[:, 0:1], ["rowi", "lo5"], "ct21")
    for i, c in enumerate((0.0, T.hi5[:, 0:1], 1.0, 0.0)):
        flat(T.ct[:, 1536 + i:2048:4], T.rowi[:, :], c, ["rowi", "hi5"], "ct3%d" % i)
    act(T.q1[:, :], T.qcol[:, :], AF.Identity, 1.0, 1.0, ["qcol"], ["q1"])
    act(T.thr[:, :], T.hi5[:, :], AF.Identity, ONE, 2 * (TWO - ONE), ["hi5"], ["thr"])
    ts(T.ct[:, 0:512:4], T.rowi[:, :], T.pcol[:, :], None, A.is_ge, None, ["rowi", "pcol"], ["ct0a"])
    ts(T.ct[:, 2:512:4], T.rowi[:, :], T.pcol[:, :], -1.0, A.is_ge, A.mult, ["rowi", "pcol"], ["ct0b"])
    for u in range(2):
        for el, c in ((1, 1.0), (3, -1.0)):
            ts(T.ct[64:128, 512 + 256 * u + el:768 + 256 * u:4], T.rowi[64:128, 64:128], T.pcol[64:128, :], c, A.is_ge, A.mult,
               ["rowi", "pcol"], ["ct1%d%d" % (u, el)])
    fill(T.pt[:, 0:1], 1.0, "pt0c")
    fill(T.pt[64:128, 1:2], 1.0, "pt1c")
    await_("v", writers["ptr"])
    fill(T.pt[:, 516:4 * W:8], 1.0, "pt2c")
    fill(T.pt[:, 512:513], 1.0 / 128, "pt3c")
    fill(T.pt[64:128, 513:514], 1.0 / 128, "pt4c")
    quant("xq", "xs", 0, 192, "xt", 0, ["xt0"], ["xq0"])
    ts(T.ct[0:1, 1027:1536:4], T.k16[0:1, :], 15.0, None, A.is_lt, None, ["k16"], ["ct23"])
    fill(T.zz[0:1, 515:4 * W:8], LIFT, "zza")
    fill(T.zz[32:33, 3:4 * W:4], 32.0, "zzb")
    await_("v", writers["ct33"])
    fill(T.ct[32:33, 1027:2048:4], 1.0, "ct4")
    ts(T.msk[:, 0:128], T.k16[:, :], T.qcol[:, :], -16.0 * LIFT, A.is_equal, A.mult, ["k16", "qcol"], ["msk"])
    quant("cq", "cqs", 0, 512, "ct", 0, ["ct0a", "ct0b", "ct0c", "ct1a", "ct1b", "ct101", "ct103", "ct111", "ct113", "ct1e", "ct4"]
          + ["ct%d%d" % (b, i) for b in (2, 3) for i in range(4)], ["cq"])
    ts(T.mk1[:, :], T.k16[:, :], T.q1[:, :], LIFT, A.is_equal, A.mult, ["k16", "q1"], ["mk1"])
    ts(T.corr[:, :], T.qcol[:, :], 15.0, LIFT, A.is_lt, A.mult, ["qcol"], ["corr"])
    fill(T.msk[:, 128:W:2], -16.0 * LIFT, "mska")
    fill(T.msk[:, 129:W:2], 0.0, "mskb")
    tt(T.msk[:, 0:128], T.msk[:, 0:128], T.mk1[:, :], A.add, ["mk1"], ["msk"])
    fill(T.nt[:, 128:512], 0.0, "nt")
    quant("adm", "adms", 0, 160, "cbt", 128, ["cbtz"], ["adm", "adms"])
    quant("ady", "adys", 0, 128, "cbt", 128, ["cbtz"], ["ady", "adys"])
    at = keys_at(0)
    for key, sl, c in (("dd0", slice(0, 40, 4), -16.0 / 512), ("dd1", slice(1, 40, 4), -2.0), ("dd2", slice(2, 40, 4), 0.0),
                       ("dd3", slice(3, 40, 20), 2.0 + 16.0 / 512), ("dd4", slice(7, 40, 20), 2.0 + 16.0 / 512 + at[0] - at[1]),
                       ("dd5", slice(11, 40, 20), 2.0 + 16.0 / 512 + at[1] - at[2]),
                       ("dd6", slice(15, 40, 20), 2.0 + 16.0 / 512 + at[2] - at[3])):
        flat(T.dd[:, sl], T.rowi[:, 0:len(range(40)[sl])], c, ["rowi"], key)
    flat(T.cc[:, 0:18:2], T.rowi[:, 0:9], 1.0, ["rowi"], "cc0")
    flat(T.cc[:, 1:14:4], T.rowi[:, 0:4], BIG, ["rowi"], "cc1")
    for h in range(2):
        act(T.dd[:, 20 * h + 17:20 * h + 18], T.qcol[:, :], AF.Identity, at[3] + (16.0 + 32 * h) / 512, 1.0 / 512,
            ["qcol", "dd1"], ["dq%d" % h])
    act(T.ncorr[:, :], T.corr[:, :], AF.Copy, 0.0, -UNIT, ["corr"], ["ncorr"])
    act(T.dist[:, :], T.rowi[:, :], AF.Abs, T.npcol[:, 0:1], 1.0, ["rowi", "npcol"], ["dist"])
    for b in range(2):
        act(T.et[:, 521 * b + 2:521 * b + 514:4], T.dist[:, :], AF.Relu, 0.25, -0.25, ["dist", "etz"], ["et%d" % b])
    await_("y", writers["ca0"])
    dma("y", T.wt[:, :], T.w[:, :], [], ["wt"], "ldw")
    dma("y", T.xt[:, 768:1536], T.x[:, 768:1536], [], ["xt1"], "ldx1")
    STEPS = ["dq0", "dq1"] + ["dd%d" % i for i in range(7)]

    def zero_block(t, i):
        quant("land%d" % t, "lans%d" % t, WIN + 128 * i, WIN + 128 * i + 128, "cbt", 128, ["cbtz"], ["lz%d%d" % (t, i)])

    def gap_constants(step):
        if step == 0:
            flat(T.cc[:, 3:16:4], T.rowi[:, 0:4], 1.0 / BIG, ["rowi"], "cc2")
            flat(T.cc[:, 17:18], T.rowi[:, 0:1], 1.0, ["rowi"], "cc3")
        else:
            flat(T.ab[:, 0:4], T.rowi[:, 0:4], FAR, ["rowi"], "ab")
            act(T.q4[:, :], T.qcol[:, :], AF.Copy, 0.0, 12.0, ["qcol"], ["q4"])
        for b in (2 * step, 2 * step + 1):
            quant("eq", "eqs", 128 * b, 128 * b + 128, "et", 520 * (b % 2) + 2 - 2 * (b // 2), ["etz", "et%d" % (b % 2)], ["eq%d" % b])

    def whole_constants(step):
        a = keys_at(PRE)
        if step == 0:
            for h in range(2):
                act(T.de[:, 20 * h:20 * h + 15], T.dd[:, 20 * h:20 * h + 15], AF.Copy, 0.0, 1.0, STEPS, ["de%d" % h])
            act(T.b0[:, :], T.corr[:, :], AF.Identity, 160.0, -257.0, ["corr"], ["b0"])
            act(T.b1[:, :], T.corr[:, :], AF.Identity, float(TOK), 1.0, ["corr"], ["b1"])
            return
        for h in range(2):
            act(T.de[:, 20 * h + 15:20 * h + 16], T.qcol[:, :], AF.Identity, 2.0 + a[2] - a[3] + (32 * h - 80.0) / 512, 1.0 / 512,
                ["qcol"], ["de%d" % (2 + h)])
        for i, (x, c) in enumerate(((16, 97.0 / 512), (17, a[3] - 1.0 / 512), (7, 2.0 + 16.0 / 512 + a[0] - a[1]),
                                    (11, 2.0 + 16.0 / 512 + a[1] - a[2]))):
            flat(T.de[:, x:40:20], T.rowi[:, 0:2], c, ["rowi"] + (["de0", "de1"] if x < 15 else []), "de%d" % (4 + i))

    zero_block(0, 0)
    XQ, CQ, EQ = ("xq", "xs"), ("cq", "cqs"), ("eq", "eqs")
    NT = ["nt0", "nt1", "nt2", "nt3"]
    for t in range(R):
        last = t == R - 1
        pre = t == PRE
        ca, cas = "ca%d" % t, "cas%d" % t
        CA = (ca, cas)
        lm, l0, meta, yo, ido = T.lm, 24 * t, T["meta%d" % t], T["yo%d" % t], T["ido%d" % t]
        land, lans, snd, sns = "land%d" % t, "lans%d" % t, "snd%d" % t, "sns%d" % t
        mm(1, XQ, 192 * t + 64, CA, 0, ["xq%d" % t, ca, cas])
        mm(0, XQ, 192 * t, CA, 0, ["xq%d" % t, ca, cas])
        scan(T.mb[64:128, :], ps(1, 0, 128, 64), T.cbt[64:128, 128:256], LOW, A.max, A.add, ["ps1", "cbtz"], ["mb"])
        scan(T.ma[:, :], ps(0, 0, 128), T.cbt[:, 128:256], LOW, A.max, A.add, ["ps0", "cbtz"], ["ma"])

        def before(q, out, m, key, p0, k0, k1, wr):
            if q == "v":
                ts(out, m[p0:128, k0:k1], m[p0:128, 127:128], None, A.is_lt, None, [key], [wr])
            else:
                act(out, m[p0:128, k0:k1], AF.Sign, m[p0:128, 127:128], -1.0, [key], [wr])

        def ranks(out, m, key, p0, wr):
            ts(out, m[p0:128, 31:96:32], m[p0:128, 127:128], 1.0 / 128, A.is_lt, A.mult, [key], [wr])
        before("s", T.pt[64:128, 5:512:4], T.mb, "mb", 64, 0, 127, "pt1")
        before("s", T.pt[64:128, 3:512:4], T.mb, "mb", 64, 0, 128, "pt3")
        ranks(T.pt[64:128, 521:538:8], T.mb, "mb", 64, "px1")
        ranks(T.pt[64:128, 515:532:8], T.mb, "mb", 64, "px3")
        before("v", T.pt[:, 4:512:4], T.ma, "ma", 0, 0, 127, "pt0")
        before("s", T.pt[:, 2:256:4], T.ma, "ma", 0, 0, 64, "pt2")
        before("v", T.pt[:, 258:512:4], T.ma, "ma", 0, 64, 128, "pt4")
        ranks(T.pt[:, 520:537:8], T.ma, "ma", 0, "px0")
        ranks(T.pt[:, 514:531:8], T.ma, "ma", 0, "px2")
        quant("pq", "pqs", 0, W, "pt", 0, ["pt", "ptr", "pt0c", "pt1c", "pt2c", "pt3c", "pt4c", "pt0", "pt1", "pt2", "pt3", "pt4",
                                           "px0", "px1", "px2", "px3"], ["pq"])
        if t == 0:
            gap_constants(0)
        else:
            zero_block(t, 0)
        if pre:
            whole_constants(0)
        mm(2, CQ, 0, ("pq", "pqs"), 0, ["cq", "pq"], W)
        mm(3, CQ, 128, ("pq", "pqs"), 0, ["cq", "pq"], W)
        act(T.zz[:, 1:4 * W:4], ps(3, 0, W), AF.Sign, T.thr[:, 0:1], -1.0, ["ps3", "thr"], ["zz1"])
        for el, c in ((0, ONE), (2, TWO)):
            ts(T.zz[:, el:4 * W:4], ps(2, 0, W), c, None, A.is_lt, None, ["ps2"], ["zz%d" % el])
        quant("zq", "zqs", 0, W, "zz", 0, ["zza", "zzb", "zz0", "zz1", "zz2"], ["zq"])
        if t == 0:
            gap_constants(1)
        if pre:
            whole_constants(1)
            zero_block(t, 1)
        mm(4, CQ, 256, ("zq", "zqs"), 0, ["cq", "zq"], W)
        mm(5, CQ, 384, ("zq", "zqs"), 0, ["cq", "zq"])
        scan(T.ls[:, 0:W], T.msk[:, 0:W], ps(4, 0, W), 0.0, A.add, A.max, ["ps4", "msk", "mska", "mskb"], ["ls0"])
        scan(T.ls[:, W:W + 128], T.msk[:, 0:128], ps(5, 0, 128), 0.0, A.add, A.max, ["ps5", "msk"], ["ls1"])
        two = [T.ls[:, W * j + 32 * far + 15:W * j + 32 * far + 32:16] for j in range(2)]

        def listed(j):
            ts(T.lst[:, j:16:2], T.ls[:, W * j + 15:W * j + 128:16], T.corr[:, 0:1], float(TOK - 1), A.subtract, A.min,
               ["ls%d" % j, "corr"], ["lst%d" % j])
        for j in range(2):
            got = T.ls[:, W * j + 15:W * j + 128:16]
            act(T.ii[:, j:16:2], got, AF.Identity, T.ncorr[:, 0:1], UNIT, ["ls%d" % j, "ncorr"], ["ii%d" % j])
            tt(T.flag[:, j:16:2], got, T.ls[:, 128:W], A.is_ge, ["ls0", "ls%d" % j], ["flag%d" % j])
            if pre:
                ts(T.pf[:, 2 * j:2 * j + 2], two[j], T.ls[:, 128 + 2 * far:129 + 2 * far], (512.0, T.b1[:, 0:1])[j], A.is_ge, A.mult,
                   ["ls0", "ls%d" % j, "b1"], ["pf%d" % j])
            else:
                listed(j)
        if pre:
            for h in range(2):
                x = 32 * far + 16 * h + 15
                ts(T.pg[:, h:h + 1], T.ls[:, x:x + 1], T.b0[:, 0:1], T.pf[:, h:h + 1], A.add, A.add, ["ls0", "b0", "pf0"], ["pg%d" % h])
            tt(T.pg[:, 2:4], two[1], T.pf[:, 2:4], A.max, ["ls1", "pf1"], ["pg2"])
        LST = ["lst0", "lst1"]
        mk = "meta%d" % t
        ark = "ark%d" % t

        def slots(kind, n):
            d = (oth + [rank])[n]
            b, x = (snd, "xq") if kind == "c" else (sns, "xs")
            o = land if kind == "c" else lans
            if n < 3:
                pick(kind, b, 64 * n, 64, x, 192 * t, 192 * t + 192, "lst", 4 * d, LST + ["xq%d" % t], ["%s.%d" % (b, n)])
            else:
                pick(kind, o, column(rank, rank, t), 64, x, 192 * t, 192 * t + 192, "lst", 4 * d, LST + ["xq%d" % t], [o + "o"])

        def place(d):
            e = senders(d, t).index(rank)
            return slice(l0 + 8 + 4 * e, l0 + 12 + 4 * e)
        tt(meta[:, :], T.ii[:, :], T.flag[:, :], A.add, ["ii0", "ii1", "flag0", "flag1"], [mk])
        if pre:
            listed(0)
            for h in range(2):
                ts(T.pv[:, h:h + 1], T.pg[:, 2 + h:3 + h], 256.0, T.pg[:, h:h + 1], A.mult, A.add, ["pg%d" % h, "pg2"], ["pv%d" % h])
            listed(1)
        for d in (oth[1:] + [far] if pre else oth):
            if pre and d == far:
                remote([d], T.pv[:, :], T.pk[:, :], "arf", ["pv0", "pv1"])
            else:
                remote([d], meta[:, 4 * d:4 * d + 4], lm[:, place(d)], "arm%d" % t, [mk])
        for n in range(int(pre), 4):
            slots("s", n)
        for n, d in enumerate(oth):
            if pre and d == far:
                continue
            me = slice(column(d, rank, t), column(d, rank, t) + 64)
            slots("c", n)
            remote([d], T[snd][:, 64 * n:64 * n + 64].bitcast(dt.uint8), T[land][:, me].bitcast(dt.uint8), ark, ["%s.%d" % (snd, n)])
            remote([d], T[sns][:, 64 * n:64 * n + 64], T[lans][:, me], ark, ["%s.%d" % (sns, n)],
                   "left" if (t, n) == (0, 2) else "sent")
        if t == 0:
            await_("y", [("left", len(full), {"left": len(full)}, "r")])
            dma("y", T.xt[:, 1536:2304], T.x[:, 1536:2304], [], ["xt2"], "ldx2")
        slots("c", 3)
        run("v", lambda e: e.tensor_copy(lm[:, l0:l0 + 4], meta[:, 4 * rank:4 * rank + 4]), [mk, "lp"], ["lo%d" % t])
        for b in range(4):
            mm(4 + b, EQ, 128 * b, CA, 0, ["eq%d" % b, ca, cas])
        act(T.hc[:, 0:384:3], (T.cbt if t == 0 else T.nt)[:, 0:128], AF.Copy, 0.0, 1.0, ["cbt"] if t == 0 else NT, ["ho"])
        for b in range(4):
            act(T.hc[:, 3 * b + 2:384:12], ps(4 + b, G * rank, G * rank + G), AF.Copy, 0.0, 2.0, ["ps%d" % (4 + b)], ["hc%d" % b])
        LM = ["lm%d" % t, "lo%d" % t, "lp"]
        DD, dd = STEPS, T.dd
        if pre:
            arrive("arf", len(common(far)), ["pk"])
            ts(T.ur[:, :], T.pk[:, :], 1.0 / 256, None, A.mult, None, ["pk"], ["ur"])
            ts(T.uf[:, :], T.pk[:, :], 256.0 * TOK + 128, None, A.is_ge, None, ["pk"], ["uf"])
            ts(T.ug[:, :], T.pk[:, :], 1.0 / 512, None, A.mult, None, ["pk"], ["ug"])
            ts(T.um[:, :], T.ur[:, :], TOK + 1.0, -0.5, A.min, A.mult, ["ur"], ["um"])
            for h in range(2):
                ts(lm[:, l0 + 17 + 2 * h:l0 + 18 + 2 * h], T.ur[:, h:h + 1], 1.0 / 512, T.uf[:, h:h + 1], A.mult, A.add,
                   ["ur", "uf", "lp"], ["lf%d" % h])
            tt(lm[:, l0 + 16:l0 + 20:2], T.ug[:, :], T.um[:, :], A.add, ["ug", "um", "lp"], ["lf2"])
            LM += ["lf0", "lf1", "lf2"]
            DD, dd = ["de%d" % i for i in range(8)], T.de
        arrive("arm%d" % t, n_meta - (len(common(far)) if pre else 0), ["lm%d" % t])
        seen = [lm[:, l0 + 2 * h:l0 + 2 * h + 18] for h in range(2)]
        for h in range(2):
            scan(T.ab[:, 4 + 2 * h:76:4], seen[h], dd[:, 20 * h:20 * h + 18], FAR, A.min, A.add, LM + DD, ["fa%d" % h])
        for h in range(2):
            scan(T.cn[:, 20 * h:20 * h + 18], seen[h], T.cc[:, 0:18], 0.0, A.add, A.mult,
                 LM + ["cc0", "cc1", "cc2", "cc3"], ["cn%d" % h])
        for h in range(2):
            tt(T.mx[:, 20 * h:20 * h + 18], seen[h], T.ab[:, 2 * h:72:4], A.max, LM + ["ab", "fa%d" % h], ["mx%d" % h])
        F, S = T.ab[:, 72:76:2], T.ab[:, 73:76:2]
        FK, SK = ["fa0", "fa1"], ["sc0", "sc1"]
        act(T.f5[:, :], F, AF.Copy, 0.0, 512.0, FK, ["f5"])
        act(T.mv[:, :], F, AF.Sign, 0.875, -1.0, FK, ["mv"])
        ts(T.alst[:, 2:4], F, 512.0, None, A.mult, None, FK, ["alst1"])
        ts(T.v2[:, :], T.cn[:, 17:40:20], 2 * PAD + 6.7, 512.0, A.is_lt, A.mult, ["cn0", "cn1"], ["v2"])
        for h in range(2):
            scan(T.ab[:, 5 + 2 * h:76:4], T.mx[:, 20 * h:20 * h + 18], dd[:, 20 * h:20 * h + 18], FAR, A.min, A.add,
                 ["mx%d" % h] + DD, ["sc%d" % h])

        def base(h):
            ts(T.blst[:, h:8:2], T.k8[:, h:8:2], T.mv[:, h:h + 1], T.q4[:, 0:1], A.add, A.add, ["k8", "mv", "q4"], ["blst%d" % h])
        base(0)
        for h in range(2):
            ts(T.alst[:, h:h + 1], T.ab[:, 73 + 2 * h:74 + 2 * h], T.v2[:, h:h + 1], T.f5[:, h:h + 1], A.mult, A.max,
               ["sc%d" % h, "v2", "f5"], ["alst0%d" % h])

        def second():
            ts(T.alst[:, 4:6], S, 512.0, None, A.mult, None, SK, ["alst2"])

        def numbers(step):
            keys = T.ab[:, 72:76]
            if step == 0:
                act(T.sg[:, :], keys, AF.Sign, 0.875, -1.0, FK + SK, ["sg"])
            elif step == 1:
                ts(T.vi[:, :], keys, 1.0 / UNIT, 2048.0 * column(rank, far, t) * pre, A.mult, A.subtract, FK + SK, ["vi"])
            elif step == 2:
                act(T.wv[:, :], T.sg[:, :], AF.Identity, 2047.5, 2048.5, ["sg"], ["wv"])
            elif step == 3:
                if pre:
                    ts(T.col[:, :], T.vi[:, :], 11, None, A.arith_shift_right, None, ["vi"], ["col"])
                ts(T.iv[:, :], T.vi[:, :], 2047, None, A.bitwise_and, None, ["vi"], ["iv"])
                if pre:
                    ts(T.z1[:, :], T.col[:, :], 0.0, float(TOK), A.max, A.min, ["col"], ["z1"])
                    tt(T.z4[:, :], T.z1[:, :], T.iv[:, :], A.add, ["z1", "iv"], ["z4"])
            else:
                tt(ido[:, :], T.wv[:, :], (T.z4 if pre else T.iv)[:, :], A.min, ["iv", "z4", "wv"], ["ido%d" % t])
                for h in range(2):
                    dma("y", T.ids[0:1, 64 * t + 32 * h:64 * t + 32 * h + 32], ido[0:16, 2 * h:2 * h + 2], ["ido%d" % t], [], "st")

        def store_y():
            mm(6, ("wq", "ws"), 0, ("ady", "adys"), 0, ["wq", "ady", "adys"])
            for i in range(2):
                act(yo[:, i:64:2], ps(6, 32 * i, 32 * i + 32), AF.Copy, 0.0, 1.0, ["ps6"], ["yo%d%d" % (t, i)])
            dma("y", T.y[:, 64 * t:64 * t + 64], yo[:, :], ["yo%d0" % t, "yo%d1" % t], [], "st")
        arrive(ark, n_tok, [land, lans])
        AL = ["alst1", "lz%d0" % t] + (["lz%d1" % t] if pre else [])
        end = 768 if pre else 640
        for i, keys in ((1, []), (0, ["alst00", "alst01"])):
            pick("c", "adm", 32 * i, 32, land, 0, end, "alst", 2 * i, AL + keys + [land, land + "o", "adm"], ["adm%d" % i])
            pick("s", "adms", 32 * i, 32, lans, 0, end, "alst", 2 * i, AL + keys + [lans, lans + "o", "adms"], ["adms%d" % i])
        base(1)

        def for_y():
            pick("c", "ady", 0, 64, land, 0, end, "alst", 2, AL + ["alst2", land, land + "o"], ["ady"])
            pick("s", "adys", 0, 64, lans, 0, end, "alst", 2, AL + ["alst2", lans, lans + "o"], ["adys"])
        if last:
            second()
            numbers(0)
        run("v", lambda e: e.tensor_copy(T.hb[:, :], T.hc[:, 0:384].indirect(T.blst[:, 0:8])),
            ["blst0", "blst1", "ho", "hc0", "hc1", "hc2", "hc3"], ["hb"])
        for i in (1, 0):
            for b in range(4):
                mm(b, EQ, 128 * b, ("adm", "adms"), 32 * i, ["eq%d" % b, "adm1", "adms1", "adm%d" % i, "adms%d" % i], part=i)
        if last:
            for_y()
            numbers(2)
            numbers(1)
        for b in range(4):
            tt(T.nt[:, b:128:4], ps(b, 0, 32), T.hb[:, 32 * b:32 * b + 32], A.add, ["ps%d" % b, "hb"], ["nt%d" % b])
            if last and b == 0:
                numbers(3)
        if last:
            numbers(4)
            store_y()
        nk = ca + "n"
        run("v", lambda e: e.quantize_mx(T[ca][:, 128:256], T[cas][:, 128:256], T.nt[:, :]), ["nt"] + NT, [nk])
        if last:
            dma("y", T.oc[:, :], T[ca][:, new].bitcast(dt.uint8), [nk], [], "st")
            for k in range(4):
                dma("y" if k == 3 else "s", T.osc[4 * k:4 * k + 4, :], T[cas][32 * k:32 * k + 4, new], [nk], [], "st")
        else:
            cn, cns = "ca%d" % (t + 1), "cas%d" % (t + 1)
            send_centroids(ca, cas, new, t + 1, nk)
            second()
            quant("xq", "xs", 192 * t + 192, 192 * t + 384, "xt", 768 * t + 768, ["xt%d" % (t + 1)], ["xq%d" % (t + 1)])
            if t + 1 == PRE:
                a, x = column(far, rank, PRE), TOK * PRE
                remote([far], T.xq[:, x:x + TOK].bitcast(dt.uint8), T["land%d" % PRE][:, a:a + TOK].bitcast(dt.uint8), "ark%d" % PRE,
                       ["xq%d" % PRE])
                remote([far], T.xs[:, x:x + TOK], T["lans%d" % PRE][:, a:a + TOK], "ark%d" % PRE, ["xq%d" % PRE])
            pick("c", cn, G * rank, G, ca, 128, 256, "ilst", 0, [nk, "ilst0", "ilst1"], [cn])
            pick("s", cns, G * rank, G, cas, 128, 256, "ilst", 0, [nk, "ilst0", "ilst1"], [cns])
            if t == 0:
                quant("wq", "ws", 0, 128, "wt", 0, ["wt"], ["wq"])
            arrive("arc%d" % (t + 1), n_cen, [cn, cns])
            await_("y", writers[cn])
            numbers(0)
            numbers(1)
            for_y()
            numbers(2)
            numbers(3)
            store_y()
            numbers(4)
    for k in cnt:
        if know["p"].get(k, 0) < cnt[k]:
            g.wait_ge(T.sem[k], cnt[k])
